import numpy as np, ml_dtypes
CORES = [24,25,26,27,28,29,30,31]
N = 8
BF = ml_dtypes.bfloat16
def gentries(a):
    return np.ascontiguousarray(a.reshape(8, 16, -1).transpose(0, 2, 1)).reshape(8, -1)
def gtable(e):
    e = np.asarray(e); return np.ascontiguousarray(e.reshape(8, -1, 16).transpose(0, 2, 1)).reshape(128, -1).astype(np.int32)
W, L, T, TH, A, B, FO = 3072, 256, 6, 64, 6, 11, 2
def parts(rng):
    return (rng.integers(0, 16, (N, 8, 16, W)), rng.integers(0, W, (N, 8, 16, W)), rng.integers(0, 64, (N, 8, 16, L)), rng.integers(0, W, (N, 8, 16, L)),
            rng.integers(0, W, (N, 8, 16, L)), rng.integers(0, 16, (N, 8, 16, L)), rng.integers(0, W, (N, 8, L)), rng.integers(0, 64, (N, 8, 16)))
def keys(x, w, p):
    z = np.take_along_axis(x, p[:, :, None, :], 3)
    return np.add.reduce(z * w[..., None], axis=2) & 63
def pack(x, d, m, u, n, q, o, w):
    return {"feat": np.ascontiguousarray(x.reshape(N, 128, W)).astype(np.float32).astype(BF), "kids": np.ascontiguousarray(d.reshape(N, 128, W)).astype(np.int32),
            "mkey": np.ascontiguousarray(m.reshape(N, 128, L)).astype(np.float32).astype(BF), "mobj": np.ascontiguousarray(u.reshape(N, 128, L)).astype(np.int32),
            "cand": np.stack([gtable(a.transpose(0, 2, 1).reshape(8, -1)) for a in n]), "want": np.ascontiguousarray(q.reshape(N, 128, L)).astype(np.float32).astype(BF),
            "last": np.ascontiguousarray(o).astype(np.int32), "wts": np.ascontiguousarray(w.reshape(N, 128, 1)).astype(np.int32)}
def setup_inputs(rng):
    return pack(*parts(rng))
def setup_inputs_corners(rng):
    x, d, m, u, n, q, o, w = parts(rng); own = np.arange(W)[None, None, None, :]
    kind = rng.integers(0, 7, (N, 8, 1, W))
    d = np.where(kind == 0, own, d); d = np.where(kind == 1, (own + 1) % W, d)
    d = np.where(kind == 2, (W - 1) * rng.integers(0, 2, d.shape), d); d = np.where(kind == 3, d[:, :, :1, :], d)
    d[2] = d[2] & -2
    x[3, :, 0] = (x[3, :, 0] & 14) | (own[0, 0] & 1); w[3] = w[3] & 62; w[3, :, 0] = w[3, :, 0] | 1
    p = rng.integers(0, W, (N, 8, L)); p[1] = 1 + np.argsort(rng.random((8, W - 2)), axis=1)[:, :L]
    p[:, :, 0] = 0; p[:, :, L - 1] = W - 1; p[3] = p[3] | 1
    n0 = n[0]; n = np.repeat(p[:, :, None, :], 16, axis=2); n[0] = np.where(rng.random((8, 1, L)) < 0.5, n0, n[0])
    j = rng.choice(np.array([0, A - 1, A, B - 1, B, 15, 16]), (N, 8, L))
    j[1] = np.where(j[1] == 16, 15, j[1]); j[2] = 16; j[3] = np.where(j[3] == 16, 0, j[3]); j[3, 7, L - 1] = 16
    c = keys(x, w, p)[:, :, None, :]; rows = np.arange(16)[None, None, :, None]; jj = j[:, :, None, :]
    off = rng.integers(1, 64, m.shape); off[3] = 2 * rng.integers(1, 32, off[3].shape)
    m = np.where((rows == jj) | ((rows > jj) & (rng.random(m.shape) < 0.2)), c, (c + off) & 63)
    m[1, :, :, 1] = c[1, :, :, 1]
    s = rng.integers(0, 5, u.shape); u = np.where(s == 0, 0, np.where(s == 1, W - 1, np.where(s == 2, p[:, :, None, :], u)))
    s = rng.integers(0, 4, o.shape); o = np.where(s == 0, 0, np.where(s == 1, W - 1, np.where(s == 2, p, o)))
    u[1, :, :, 1] = rng.integers(1, W - 1, (8, 16)); u[1, :, :, L - 1] = rng.integers(1, W - 1, (8, 16))
    z = np.take_along_axis(x[1], p[1][:, None, :], 2)
    q[1, 6] = z[6]; q[1, 7] = np.where(z[7] >= 8, 0, 15); u[1, 6, 0, 0] = W - 1; o[1, 6, 0] = 0
    return pack(x, d, m, u, n, q, o, w)
def setup_inputs_ends(rng):
    x, d, m, u, n, q, o, w = parts(rng)
    x = 15 * (rng.random((N, 8, 16, W)) < rng.choice(np.array([0.0, 0.3, 0.5, 0.5, 0.7, 1.0]), (N, 8, 1, W))).astype(np.int64)
    for g in range(8):
        x[:, g, :, 0] = 15 * (g & 1); x[:, g, :, W - 1] = 15 * (g & 1)
        x[:, g, :, W - 2] = 15 * (g & 1); x[:, g, 15, W - 2] = 15 - 15 * (g & 1)
    w = 63 * rng.integers(0, 2, w.shape); w[:, 6:] = 63; w[:, 0] = 0
    q = 15 * rng.integers(0, 2, q.shape)
    d = np.where(rng.random(d.shape) < 0.7, (W - 1) * rng.integers(0, 2, d.shape), d)
    n = np.where(rng.random(n.shape) < 0.7, (W - 1) * rng.integers(0, 2, n.shape), n)
    u = np.where(rng.random(u.shape) < 0.7, (W - 1) * rng.integers(0, 2, u.shape), u)
    o = np.where(rng.random(o.shape) < 0.75, (W - 1) * rng.integers(0, 2, o.shape), o)
    m = np.where(rng.random(m.shape) < 0.7, 63 * rng.integers(0, 2, m.shape), (49 * rng.integers(0, 17, m.shape)) & 63)
    for l in (0, 1, 2, 3, L - 4, L - 3, L - 2, L - 1): n[:, :, 0::2, l] = W - 1; n[:, :, 1::2, l] = 0
    for l, k in ((2, 1), (3, 13), (L - 4, 1), (L - 3, 13)): n[:, :, k, l] = W - 2; n[:, :, 14, l] = W - 2
    for g in range(8):
        for l in (1, 2, 3, L - 4, L - 3, L - 1): q[:, g, :, l] = 15 - 15 * (g & 1)
        for l in (0, L - 2): q[:, g, :, l] = 15 * (g & 1)
    kk = keys(x, w, np.full((N, 8, 1), W - 1))
    m[:, :, 12:, L - 1] = 63; u[:, :, 12:, L - 1] = W - 1
    m[:, :, 11, 1] = kk[:, :, 0]; m[:, :, 11, L - 1] = kk[:, :, 0]
    h = W // FO
    d[:, 7, 15, h - 1::h] = W - 1; d[:, 7, 15, h - 2::h] = W - 1; d[:, :, 0, 0::h] = 0
    return pack(x, d, m, u, n, q, o, w)
def setup_inputs_shared(rng):
    x, d, m, u, n, q, o, w = parts(rng)
    hot = np.stack([np.concatenate([np.array([0, W - 1]), 1 + rng.permutation(W - 2)[:22]]) for g in range(8)])
    gg = np.arange(8)[None, :, None, None]
    d = hot[gg, rng.integers(0, 24, d.shape)]; n = hot[gg, rng.integers(0, 24, n.shape)]
    u = np.where(rng.random(u.shape) < 0.5, hot[gg, rng.integers(0, 24, u.shape)], u)
    kh = keys(x, w, np.repeat(hot[None], N, axis=0))
    m = np.where(rng.random(m.shape) < 0.6, kh[np.arange(N)[:, None, None, None], gg, rng.integers(0, 24, m.shape)], m)
    for r, g, i in ((0, 0, 2), (N - 1, 7, 1)):
        n[r, g] = hot[g, i]; m[r, g, 0] = kh[r, g, i]; u[r, g, 0, 0] = hot[g, 3]
    return pack(x, d, m, u, n, q, o, w)
def setup_inputs_spread(rng):
    x, d, m, u, n, q, o, w = parts(rng)
    def uneven(top, shape, kshape):
        return np.minimum((top * rng.random(shape) ** np.exp2(rng.integers(-2, 3, kshape))).astype(np.int64), top - 1)
    x = uneven(16, x.shape, (N, 8, 1, W)); q = uneven(16, q.shape, (N, 8, 1, L)); d = uneven(W, d.shape, (N, 8, 16, 1))
    u = uneven(W, u.shape, (N, 8, 1, L)); n = uneven(W, n.shape, (N, 8, 16, 1)); o = uneven(W, o.shape, (N, 8, 1)); w = uneven(64, w.shape, (N, 8, 1))
    m = m & rng.choice(np.array([63, 63, 7, 56, 1]), (N, 8, 1, L))
    return pack(x, d, m, u, n, q, o, w)
def setup_inputs_ties(rng):
    x, d, m, u, n, q, o, w = parts(rng); h = W // 2
    x[..., h:] = x[..., :h][..., ::-1]
    p = rng.integers(0, W, (N, 8, L)); p[:, :, L - 1] = W - 1
    z = np.take_along_axis(x, p[:, :, None, :], 3); tot = TH + rng.integers(-1, 2, (N, 8, 1, L))
    dl = (tot >> 4) + (np.arange(16)[None, None, :, None] < (tot & 15))
    q = np.where(z >= 8, z - dl, z + dl)
    twin = np.where(rng.random(n.shape) < 0.5, p[:, :, None, :], W - 1 - p[:, :, None, :])
    n = np.where(rng.random(n.shape) < 0.6, twin, n)
    c = keys(x, w, p)[:, :, None, :]
    m = np.where(rng.random((N, 8, 1, L)) < 0.4, (c + (m & 3)) & 63, m)
    return pack(x, d, m, u, n, q, o, w)
def check_inputs(d):
    bad = []
    for k, lo, hi in (("feat", 0, 15), ("kids", 0, W - 1), ("mkey", 0, 63), ("mobj", 0, W - 1), ("cand", 0, W - 1), ("want", 0, 15), ("last", 0, W - 1), ("wts", 0, 63)):
        v = np.asarray(d[k]).astype(np.float64)
        if not (np.min(v) >= lo and np.max(v) <= hi and np.all(v == np.rint(v))): bad.append("range of " + k)
    return bad
def reference(feat, kids, mkey, mobj, cand, want, last, wts):
    x = np.ascontiguousarray(feat.astype(np.int32).reshape(N, 8, 16, W).transpose(0, 1, 3, 2))
    d = np.array(kids.astype(np.int64).reshape(N, 8, 16, W).transpose(0, 1, 3, 2))
    m = np.array(mkey.astype(np.int64).reshape(N, 8, 16, L).transpose(0, 1, 3, 2))
    u = np.array(mobj.astype(np.int64).reshape(N, 8, 16, L).transpose(0, 1, 3, 2))
    n = np.stack([gentries(a) for a in cand]).astype(np.int64).reshape(N, 8, L, 16)
    q = np.array(want.astype(np.int32).reshape(N, 8, 16, L).transpose(0, 1, 3, 2))
    prev = np.array(last.astype(np.int64)); w = wts.astype(np.int64).reshape(N, 8, 1, 16)
    count = np.zeros(N, np.int64); gi = np.arange(8)[:, None]
    for t in range(T):
        seen = np.zeros(N, np.int64)
        for r in range(N):
            s = (r + t) % N
            dist = np.add.reduce(np.abs(x[s][gi[:, :, None], n[r]] - q[r][:, :, None, :]), axis=3)
            like = dist < TH + (count[s] & 15); alike = np.any(like, axis=2)
            k = np.where(alike, np.argmax(like, axis=2), np.argmin(dist, axis=2))
            o = np.take_along_axis(n[r], k[:, :, None], 2)[:, :, 0]
            xo = x[s][gi, o]; c = np.add.reduce(xo * w[s], axis=2) & 63
            hit = m[s] == c[:, :, None]; covered = np.any(hit, axis=2); j = np.argmax(hit, axis=2)
            own = d[s][gi, o]; e = d[s][gi, np.take_along_axis(u[s], j[:, :, None], 2)[:, :, 0]]
            top = covered & (j < B); low = covered & ((j < A) | (j >= B))
            new = np.concatenate([np.where(top[:, :, None], e[:, :, :8], own[:, :, :8]), np.where(low[:, :, None], e[:, :, 8:], own[:, :, 8:])], axis=2)
            g, l = np.nonzero(covered); first = np.unique(g * W + o[g, l], return_index=True)[1]
            g, l = g[first], l[first]; d[s, g, o[g, l]] = new[g, l]
            g, l = np.nonzero(~alike); row = (l + 5 * t) & 15
            m[s, g, l, row] = c[g, l]; u[s, g, l, row] = prev[r, g, l]
            seen[s] = np.count_nonzero(covered); prev[r] = o; n[r] = new; q[r] = np.abs(q[r] - xo)
        count = seen
    dd = d.transpose(0, 1, 3, 2).reshape(N, 128, FO, W // FO)
    return {"yn": n.transpose(0, 1, 3, 2).reshape(N, 128, L).astype(np.float32), "ymu": (64 * u + m).transpose(0, 1, 3, 2).reshape(N, 128, L).astype(np.float32),
            "yd": np.add.reduce(dd * np.arange(1, FO + 1)[:, None], axis=2).astype(np.float32)}

@@ -1,0 +1,605 @@
+from concourse.mybir import AluOpType, AxisListType, ActivationFunctionType
+
+W, L, STEPS = 3072, 256, 6
+MAGIC = 12582912.0
+SCH = (184, 256)
+VCH = [(0, 64), (64, 128), (128, 184)]
+NVL = SCH[0]
+BIG = 1000000.0
+
+SCRATCH = {}
+
+
+def _buffers():
+    for dtype, names in (
+        ("float32", "colf 256 cmf 256 cgf 128 pcol 40 m16 16 w16 16 mw16 16 ct1 128 ct2 128 ct3 128 onef 128 rst 256 dump 16 "
+                    "t64 64 t64b 64 t64c 64 tba 48 tbb 64 kc 256 comp 256 tr 256 sc 256 r16 16 ka 256 kb 256 new 256 ctv 16 cs 1 "
+                    "lim 2 odm 16 wt1 16 wt2 16 my 256 my2 256 yl 256 ydb 1536"),
+        ("bfloat16", "featb 3072 keytab 3072 ntab 3072 tb 3072 mk 256 ident 128 nident 128 selp 144 sumb 144 blk 128 nblk 128 "
+                     "blk8 8 pre 128 rs 128 tri 128 onesg 240 nbias 128 oneb 512 kwf 128 wx 4096 d 4096 da 4096 fs 2048 dm 256 "
+                     "hit 256 fi 256 sel 256 nsel 256 xo 256 code 256 le 256 lo 256 eq 3072 wr 256 nus 256 mt1 256"),
+        ("float16", "last16 256 i16 128 sumf 144 sper 512 g8 144 rot 768 ej 2048 od 32 fe 256 pv 16 nap 32 nr 32 mt2 256"),
+        ("int32", "candi 256 kt 3328 mobi 256 lasti 256 wti 1 pint 16 cint 2"),
+        ("uint16", "el 16 wo 16"),
+    ):
+        words = names.split()
+        for k in range(0, len(words), 2):
+            SCRATCH[words[k]] = ("sbuf", [128, int(words[k + 1])], dtype)
+    for t in range(STEPS):
+        SCRATCH["cw%d" % t] = ("sbuf", [128, 272], "uint16")
+        SCRATCH["co%d" % t] = ("sbuf", [128, 272], "uint16")
+        SCRATCH["wt_%d" % t] = ("sbuf", [128, 256], "bfloat16")
+        if t < STEPS - 1:
+            SCRATCH["wn%d" % t] = ("sbuf", [128, 256], "bfloat16")
+    for b in range(8):
+        SCRATCH["b%d" % b] = ("psum", [128, 512], "float32")
+
+
+_buffers()
+LOADS = ["cand", "feat0", "feat1", "feat2", "want", "wts", "last", "mkey", "mobj", "kids"]
+SEMAPHORES = ["sv", "ss", "sp", "sg", "lsem", "arry", "oyn", "omu"] + ["ld_" + x for x in LOADS] + ["oyd%d" % k for k in range(3)]
+SEMAPHORES += ["arrw%d" % k for k in range(1, STEPS)] + ["arrc%d" % k for k in range(1, STEPS)]
+
+
+def A(name, c0, c1, step=1, p0=0, p1=128):
+    return (name, p0, p1, c0, c1, step)
+
+
+def overlap(a, b):
+    if a[1] >= b[2] or b[1] >= a[2] or a[3] >= b[4] or b[3] >= a[4]:
+        return False
+    if a[5] > 1 and a[5] == b[5] and (a[3] - b[3]) % a[5]:
+        return False
+    return True
+
+
+def covers(a, b):
+    return a[5] == 1 and a[1] <= b[1] and a[2] >= b[2] and a[3] <= b[3] and a[4] >= b[4]
+
+
+def machine(g, T):
+    q = {"V": g.vector, "S": g.scalar, "P": g.tensor, "G": g, "Y": g.sync}
+    sem = {"V": "sv", "S": "ss", "P": "sp", "G": "sg"}
+    count = {}
+    clock = {e: {} for e in q}
+    hist = {}
+
+    def need(e, ent):
+        s, v, ck = ent[3], ent[4], ent[5]
+        mine = clock[e]
+        if mine.get(s, 0) < v:
+            q[e].wait_ge(T.sem[s], v)
+            for k in ck:
+                if mine.get(k, 0) < ck[k]:
+                    mine[k] = ck[k]
+            if mine.get(s, 0) < v:
+                mine[s] = v
+
+    def order(e, R, Wr):
+        found = []
+        for regs, w in ((R, False), (Wr, True)):
+            for r in regs:
+                psum = r[0][0] == "b" and r[0][1:].isdigit()
+                for ent in hist.get(r[0], []):
+                    if (psum and ent[2] != e) or ((w or ent[1]) and overlap(r, ent[0])):
+                        found.append(ent)
+        found.sort(key=lambda ent: -ent[4])
+        for ent in found:
+            need(e, ent)
+
+    def log(e, R, Wr, s, v):
+        ck = dict(clock[e])
+        for regs, w in ((R, False), (Wr, True)):
+            for r in regs:
+                h = hist.setdefault(r[0], [])
+                if w:
+                    h[:] = [x for x in h if not covers(r, x[0])]
+                h[:] = [x for x in h if not (x[2] == e and x[3] == s and x[0] == r and x[1] == w)]
+                h.append([r, w, e, s, v, ck])
+
+    def ap(x):
+        if x[0] == "ind":
+            return ap(x[1]).indirect(ap(x[2]))
+        t = T[x[0]]
+        if x[5] == 1:
+            return t[x[1]:x[2], x[3]:x[4]]
+        return t[x[1]:x[2], x[3]:x[4]:x[5]]
+
+    def run(e, call, R, Wr, acc=False):
+        R2, W2 = [], []
+        for x in R:
+            if isinstance(x, tuple):
+                R2 += [x[1], x[2]] if x[0] == "ind" else [x]
+        for x in Wr:
+            if x[0] == "ind":
+                W2.append(x[1])
+                R2.append(x[2])
+            else:
+                W2.append(x)
+        order(e, R2, [] if acc else W2)
+        if acc:
+            for x in W2:
+                for ent in hist.get(x[0], []):
+                    if ent[2] != e:
+                        need(e, ent)
+        s = sem[e]
+        count[s] = count.get(s, 0) + 1
+        call().then_inc(T.sem[s], 1)
+        log(e, R2, W2, s, count[s])
+
+    def sc(x):
+        return ap(x) if isinstance(x, tuple) else x
+
+    def tt(out, a, b, op):
+        run("V", lambda: g.vector.tensor_tensor(ap(out), ap(a), ap(b), op), [a, b], [out])
+
+    def ts(out, a, s1, op0, s2=None, op1=None):
+        if op1 is None:
+            run("V", lambda: g.vector.tensor_scalar(ap(out), ap(a), sc(s1), None, op0), [a, s1], [out])
+        else:
+            run("V", lambda: g.vector.tensor_scalar(ap(out), ap(a), sc(s1), sc(s2), op0, op1), [a, s1, s2], [out])
+
+    def cp(out, a):
+        run("V", lambda: g.vector.tensor_copy(ap(out), ap(a)), [a], [out])
+
+    def fill(out, c):
+        run("V", lambda: g.vector.memset(ap(out), c), [], [out])
+
+    def red(out, a):
+        run("V", lambda: g.vector.tensor_reduce(ap(out), ap(a), AxisListType.X, AluOpType.add), [a], [out])
+
+    def scan(out, d0, d1, init, op0, op1):
+        run("V", lambda: g.vector.tensor_tensor_scan(ap(out), ap(d0), ap(d1), init, op0, op1), [d0, d1], [out])
+
+    def tr(out, a):
+        run("V", lambda: g.vector.transpose(ap(out), ap(a)), [a], [out])
+
+    def act(out, a, func, bias=0.0, scale=1.0, acc=None):
+        if acc is None:
+            run("S", lambda: g.scalar.activation(ap(out), ap(a), func, bias=sc(bias), scale=sc(scale)), [a, bias, scale], [out])
+        else:
+            run("S", lambda: g.scalar.activation(ap(out), ap(a), func, bias=sc(bias), scale=sc(scale), accum_out=ap(acc)),
+                [a, bias, scale], [out, acc])
+
+    def mm(out, lhsT, rhs, start=True, stop=True):
+        run("P", lambda: g.tensor.matmul(ap(out), ap(lhsT), ap(rhs), start, stop), [lhsT, rhs], [out], acc=not start)
+
+    def iota(out, pattern, base, cm, small=True):
+        if small:
+            run("G", lambda: g.iota(ap(out), pattern, base, cm, allow_small_or_imprecise_dtypes=True), [], [out])
+        else:
+            run("G", lambda: g.iota(ap(out), pattern, base, cm), [], [out])
+
+    def pick(out, a, op, base, cm, step, n):
+        run("G", lambda: g.affine_select(ap(out), ap(a), [[step, n]], op, 0.0, base, cm), [a], [out])
+
+    def pick2(out, a, pattern):
+        run("G", lambda: g.affine_select(ap(out), ap(a), pattern, AluOpType.is_equal, 0.0, 0, 0), [a], [out])
+
+    def load(e, out, src, s):
+        q[e].dma_start(ap(out), src).then_inc(T.sem[s], 16)
+        hist.setdefault(out[0], []).append([out, True, "D", s, 16, {}])
+
+    def store(e, dst, a, s):
+        order(e, [a], [])
+        q[e].dma_start(dst, ap(a)).then_inc(T.sem[s], 16)
+        count[s] = 16
+
+    def landed(out, s, v):
+        hist.setdefault(out[0], []).append([out, True, "R", s, v, {}])
+
+    def send(a, out, s, addr, mask, n):
+        order("G", [a], [])
+        g.remote_dma(ap(out), ap(a), T.sem[s], T.sem["lsem"], addr[1], addr[0], mask)
+        count["lsem"] = count.get("lsem", 0) + n
+
+    def finish(extra):
+        for s, v in list(count.items()) + extra:
+            if clock["G"].get(s, 0) < v:
+                g.wait_ge(T.sem[s], v)
+
+    return dict(tt=tt, ts=ts, cp=cp, fill=fill, red=red, scan=scan, tr=tr, act=act, mm=mm, iota=iota, pick=pick, pick2=pick2, load=load,
+                store=store, landed=landed, send=send, finish=finish)
+
+
+def rank_program(g, core, T, topo):
+    rank = T.rank_of(core)
+    if rank is None:
+        return
+    O, F = AluOpType, ActivationFunctionType
+    m = machine(g, T)
+    tt, ts, cp, fill, red, scan, tr, act, mm, iota, pick = (
+        m[k] for k in ("tt", "ts", "cp", "fill", "red", "scan", "tr", "act", "mm", "iota", "pick"))
+    n = len(T.cores)
+    nxt, home = T.cores[(rank + 1) % n], T.cores[(rank - STEPS + 1) % n]
+
+    def link(dst):
+        return topo.addr(dst), topo.mask(core, dst), len(topo.engines(core, dst))
+
+    def full(name, w=128):
+        return A(name, 0, w)
+
+    load = m["load"]
+    load("S", full("wti", 1), T.wts[:, :], "ld_wts")
+    load("Y", full("candi", 256), T.cand[:, :], "ld_cand")
+    load("S", full("wt_0", 256), T.want[:, :], "ld_want")
+    for k in range(3):
+        load("Y", A("featb", 1024 * k, 1024 * k + 1024), T.feat[:, 1024 * k:1024 * k + 1024], "ld_feat%d" % k)
+    load("S", A("lasti", 0, 256, 1, 0, 8), T.last[:, :], "ld_last")
+    load("S", full("mk", 256), T.mkey[:, :], "ld_mkey")
+    load("S", full("mobi", 256), T.mobj[:, :], "ld_mobj")
+    load("Y", A("kt", 0, W), T.kids[:, :], "ld_kids")
+
+    iota(full("pint", 1), [[0, 1]], 0, 1, False)
+    iota(full("cgf", 128), [[1, 8], [0, 16]], 0, 0)
+    iota(full("colf", 256), [[1, 256]], 0, 0)
+    iota(full("oneb", 128), [[0, 128]], 1, 0)
+    pick(full("ident"), full("oneb"), O.is_equal, 0, 1, -1, 128)
+    iota(full("cmf", 256), [[0, 16], [1, 16]], 0, 0)
+    iota(A("oneb", 128, 256), [[0, 128]], -1, 0)
+    pick(full("nident"), A("oneb", 128, 256), O.is_equal, 0, 1, -1, 128)
+    iota(A("oneb", 256, 384), [[0, 128]], -16, 0)
+    pick(full("tri"), A("oneb", 256, 384), O.is_ge, 0, 1, -1, 128)
+
+    iota(full("sc", 256), [[0, 256]], int(BIG), 0)
+    run_pick = m["pick2"]
+    run_pick(full("rst", 256), full("sc", 256), [[0, 16], [1, 16]])
+
+    def pi(k):
+        return A("pint", k, k + 1)
+
+    def pc(k):
+        return A("pcol", k, k + 1)
+    PF, PM, PG, P16, P1615, HA, HB, PP16, PM16, KCOL, CA, CB, PARE, PARO, BS, MA, MB, WF, WF64, G15 = range(20)
+    PR = 24
+    ts(pi(2), pi(0), 4, O.arith_shift_right)
+    ts(pi(1), pi(0), 15, O.bitwise_and)
+    cp(pc(PG), pi(2))
+    cp(pc(PM), pi(1))
+    cp(pc(PF), pi(0))
+    ts(full("blk"), full("cgf"), pc(PG), O.is_equal, 1.0, O.mult)
+    ts(pc(P1615), pc(PG), 16.0, O.mult, 15.0, O.add)
+    ts(full("selp", 143), full("colf", 143), pc(P1615), O.is_equal, 16.0, O.mult)
+
+    def build_wx(t):
+        for k in range(16):
+            out, src = A("wx", k, 16 * NVL, 16), A("wt_%d" % t, 0, NVL)
+            if t and k >= 16 - GWX:
+                pick(out, src, O.is_ge, 1, 0, 0, NVL)
+            else:
+                cp(out, src)
+
+    def key_a(k):
+        b, c, x, z = A("b%d" % k, 0, 512), A("featb", 512 * k, 512 * k + 512), A("ntab", 512 * k, 512 * k + 512), A("kf", 512 * k, 512 * k + 512)
+        if k < 3:
+            mm(b, full("kwf"), c)
+            act(z, b, F.Copy, bias=-31.5)
+        else:
+            z = b
+            mm(b, full("kwf"), c, True, False)
+            mm(b, A("nbias", 0, 128, 1, 0, 1), A("nbone", 0, 512, 1, 0, 1), False, True)
+        ts(x, z, 64.0 * MAGIC, O.add, 64.0 * MAGIC, O.subtract)
+
+    def key_b(k):
+        b, c, x = A("b%d" % k, 0, 512), A("featb", 512 * k, 512 * k + 512), A("ntab", 512 * k, 512 * k + 512)
+        mm(b, full("kwf"), c, True, False)
+        mm(b, full("nident"), x, False, True)
+        act(A("keytab", 512 * k, 512 * k + 512), b, F.Copy)
+
+    def consts1():
+        ts(pc(KCOL), pc(PM), 0.625, O.add)
+        fill(A("lim", 0, 1), -1008.0)
+        ts(pi(3), pi(0), 16, O.bitwise_and)
+        ts(pc(PP16), pc(PF), 16.0, O.add)
+        ts(pc(PM16), pc(PF), -16.0, O.add)
+        ts(pc(HB), pi(3), 256.0, O.mult)
+        ts(pc(HA), pc(HB), -1.0, O.mult, 4096.0, O.add)
+        ts(A("sper", 256, 384), full("colf"), pc(PM16), O.is_equal, pc(HB), O.mult)
+        ts(A("sper", 384, 512), full("colf"), pc(PF), O.is_equal, pc(HB), O.mult)
+        ts(A("sper", 0, 128), full("colf"), pc(PF), O.is_equal, pc(HA), O.mult)
+        ts(A("sper", 128, 256), full("colf"), pc(PP16), O.is_equal, pc(HA), O.mult)
+
+    def consts_bits():
+        ts(full("m16", 16), full("colf", 16), pc(PM), O.is_equal, 1.0, O.mult)
+        fill(full("t64c", 16), 0.5)
+        fill(full("t64b", 16), 0.0)
+        scan(full("w16", 16), full("t64c", 16), full("t64b", 16), 1.0, O.mult, O.add)
+        tt(full("mw16", 16), full("m16", 16), full("w16", 16), O.mult)
+        ts(pc(MB), pc(PM), 6.0, O.is_lt)
+        ts(pc(CA), pc(PM), 12.0, O.is_lt)
+        red(pc(BS), full("mw16", 16))
+        tt(pc(MA), pc(CA), pc(MB), O.subtract)
+        for mul, k, out, mask in ((64.0, 48, "tba", MA), (1.0, 64, "tbb", MB)):
+            ts(full("t64", k), full("colf", k), mul, O.mult, 0.5, O.add)
+            ts(full("t64", k), full("t64", k), pc(BS), O.mult)
+            ts(full("t64b", k), full("t64", k), MAGIC, O.add, MAGIC, O.subtract)
+            tt(full("t64c", k), full("t64", k), full("t64b", k), O.subtract)
+            ts(full("t64c", k), full("t64c", k), 0.0, O.is_gt, 2.0, O.mult)
+            ts(full(out, k), full("t64c", k), -1.0, O.add, pc(mask), O.mult)
+
+    def bit_table(k0, k1):
+        for k in range(k0, k1):
+            act(A("tb", 64 * k, 64 * k + 64), full("tbb", 64), F.Identity, bias=A("tba", k, k + 1))
+
+    def consts2():
+        ts(full("ct1"), A("cmf", 0, 128), pc(PM), O.is_gt, 2.0, O.mult)
+        ts(full("ct2"), A("cmf", 0, 128), pc(PM), O.is_equal, 1.0, O.mult)
+        ts(pc(CA), pc(PM), 11.0, O.is_lt)
+        tt(full("ct3"), full("ct1"), full("ct2"), O.subtract)
+        ts(pc(CB), pc(PM), 6.0, O.is_lt)
+        tt(full("pre"), full("ct3"), full("blk"), O.mult)
+        ts(full("sumf", 143), full("colf", 143), pc(P1615), O.is_equal, 1.0, O.mult)
+        tt(pc(CB), pc(CB), pc(CA), O.subtract)
+        ts(A("b7", 0, 256), full("mobi", 256), -1536.0, O.add)
+        ts(pc(CB), pc(CB), 1.0, O.add)
+        ts(full("ct1"), A("cmf", 0, 128), 8.0, O.is_lt)
+        tt(pc(CA), pc(CA), pc(CB), O.subtract)
+        ts(full("ct2"), full("ct1"), pc(CA), O.mult, pc(CB), O.add)
+        ts(full("blk8", 8), full("colf", 8), pc(PG), O.is_equal, 1.0, O.mult)
+        ts(pi(4), pi(2), 1, O.bitwise_and)
+        tt(full("rs"), full("ct2"), full("blk"), O.mult)
+        ts(pc(PARO), pi(4), 1.0, O.mult)
+        ts(pc(PARE), pc(PARO), -1.0, O.mult, 1.0, O.add)
+
+    def consts3():
+        ts(full("dump", 16), full("colf", 16), 16.0, O.mult, pc(PM), O.add)
+        ts(full("dump", 16), full("dump", 16), 1536.0, O.add)
+        ts(full("nblk"), full("blk"), -1.0, O.mult)
+        ts(full("i16"), full("colf"), pc(PF), O.is_equal, 1.0, O.mult)
+        fill(full("onesg", 240), 0.0)
+        fill(A("onesg", 112, 128), 1.0)
+        fill(full("onef"), 1.0)
+        ts(A("last16", 0, 256, 1, 0, 8), A("lasti", 0, 256, 1, 0, 8), -1536.0, O.add)
+        ts(pc(G15), pc(PF), 16.0, O.mult, 15.0, O.add)
+        ts(A("g8", 0, 143, 1, 0, 8), A("colf", 0, 143, 1, 0, 8), A("pcol", G15, G15 + 1, 1, 0, 8), O.is_equal, 1.0, O.mult)
+        for k in range(16):
+            mm(A("b6", 96, 112), A("g8", 15 - k, 143 - k, 1, 0, 8), A("last16", k, 256, 16, 0, 8), k == 0, k == 15)
+        ts(full("sumb", 143), full("colf", 143), pc(P1615), O.is_equal, 1.0, O.mult)
+        fill(A("kt", W, W + L), 0)
+        cp(full("pv", 16), A("b6", 96, 112))
+        ts(pc(P16), pc(PG), 16.0, O.mult)
+        for k in range(16):
+            ts(A("ej", 128 * k, 128 * k + 128), full("i16"), A("m16", k, k + 1), O.mult)
+
+    def const_rot(t):
+        ts(pi(5), pi(1), float(5 * t), O.add)
+        ts(pi(6), pi(5), 15, O.bitwise_and)
+        tt(pc(PR + t), pi(6), pc(P16), O.add)
+        ts(A("rot", 128 * t, 128 * t + 128), full("colf"), pc(PR + t), O.is_equal, 1.0, O.mult)
+
+    consts_bits()
+    ts(pc(WF), full("wti", 1), 1.0, O.mult)
+    ts(full("kwf"), full("blk"), pc(WF), O.mult)
+    cp(A("cw0", 0, 256), full("candi", 256))
+    build_wx(0)
+    consts1()
+    fill(A("nbias", 0, 128, 1, 0, 1), -31.5)
+    fill(A("nbone", 0, 512, 1, 0, 1), 1.0)
+
+    def keytable(k0, k1):
+        for k in range(k0, k1):
+            if k < 6:
+                key_a(k)
+            if k:
+                key_b(k - 1)
+    key_a(0)
+    key_a(1)
+    bit_table(0, 26)
+    key_b(0)
+    keytable(2, KEY0)
+    FEAT, KEYS, BITS = full("featb", W), full("keytab", W), full("tb", W)
+    KIDS, KALL = A("kt", 0, W), A("kt", 0, W + L)
+    late = {}
+
+    def dist_to(l0, l1):
+        return A("b4", l0, l1) if l1 <= 128 else A("b5", l0 - 128, l1 - 128)
+
+    for t in range(STEPS):
+        cw, wt, co = "cw%d" % t, "wt_%d" % t, "co%d" % t
+        final = t == STEPS - 1
+        OL = A(co, 256, 272)
+        s0, s1 = SCH
+        sw = s1 - s0
+        kb = 512 // sw
+        act(A("fs", 0, 16 * sw), ("ind", FEAT, A(cw, s0, s1)), F.Copy)
+        for l0, l1 in VCH:
+            r = A("d", 16 * l0, 16 * l1)
+            tt(r, ("ind", FEAT, A(cw, l0, l1)), A("wx", 16 * l0, 16 * l1), O.subtract)
+            if t == 0 and l0 == 0:
+                keytable(KEY0, 7)
+        ts(full("kc", 256), A(cw, 0, 256), 1.0 / 4096.0, O.mult, pc(KCOL), O.add)
+        def abs_v(l0, l1):
+            act(A("da", 16 * l0, 16 * l1), A("d", 16 * l0, 16 * l1), F.Abs)
+            for k in range(16):
+                mm(dist_to(l0, l1), A("selp", 15 - k, 143 - k), A("da", 16 * l0 + k, 16 * l1, 16), k == 0, k == 15)
+        for k in range(16):
+            c = A("b%d" % (k // kb), (k % kb) * sw, (k % kb) * sw + sw)
+            mm(c, full("nident"), A(wt, s0, s1), True, False)
+            mm(c, full("ident"), A("fs", k, 16 * sw, 16), False, True)
+        abs_v(*VCH[0])
+        if t:
+            late["w"]()
+        for k in range(0, 16, kb):
+            e = min(k + kb, 16)
+            act(A("da", 16 * s0 + sw * k, 16 * s0 + sw * e), A("b%d" % (k // kb), 0, sw * (e - k)), F.Abs)
+        for k in range(16):
+            mm(dist_to(s0, s1), A("selp", 15 - k, 143 - k), A("da", 16 * s0 + sw * k, 16 * s0 + sw * k + sw), k == 0, k == 15)
+        if t:
+            late["scatter"]()
+        for c in VCH[1:]:
+            abs_v(*c)
+        act(A("b6", 0, 128), A("b4", 0, 128), F.Relu, bias=A("lim", 0, 1))
+        if t:
+            ts(full("pv", 16), A(cw, 256, 272), -1536.0, O.add)
+            late["mount0"]()
+        act(A("b3", 0, 128), A("b5", 0, 128), F.Relu, bias=A("lim", 0, 1))
+        if t == 0:
+            bit_table(26, 48)
+            consts2()
+        for h in range(2):
+            a, b = 128 * h, 128 * h + 128
+            if t and h:
+                late["mount1"]()
+                late["mount2"]()
+            tt(A("comp", a, b), A("b3", 0, 128) if h else A("b6", 0, 128), A("kc", a, b), O.add)
+            tr(A("tr", a, b), A("comp", a, b))
+            scan(A("sc", a, b), A("rst", a, b), A("tr", a, b), BIG, O.max, O.min)
+        best = A("sc", 15, 256, 16)
+        ts(full("r16", 16), best, MAGIC, O.add, MAGIC, O.subtract)
+        ts(A("od", 16, 32), best, 16.5, O.is_ge, 1.0 / 4096.0, O.mult)
+        tt(A("od", 0, 16), best, full("r16", 16), O.subtract)
+        for dd in range(2):
+            for bb in range(2):
+                k = 2 * dd + bb
+                mm(A("b6", dd, 32, 2), A("sper", 128 * k, 128 * k + 128), A("od", bb, 32, 2), bb == 0, bb == 1)
+        ts(OL, A("b6", 0, 16), 1536.0, O.add)
+        tt(full("dm", 256), ("ind", KEYS, OL), full("mk", 256), O.subtract)
+        if not final:
+            act(full("xo", 256), ("ind", FEAT, OL), F.Copy)
+        act(full("code", 256), ("ind", BITS, OL), F.Copy)
+        ts(full("hit", 256), full("dm", 256), 0.0, O.is_equal)
+        mm(A("b5", 0, 256), full("pre"), full("hit", 256))
+        ts(full("fi", 256), A("b5", 0, 256), 0.0, O.is_lt)
+        if not final:
+            mm(A("b0", 0, 256), full("ident"), A(wt, 0, 256), True, False)
+            mm(A("b0", 0, 256), full("nident"), full("xo", 256), False, True)
+            act(A("wn%d" % t, 0, 256), A("b0", 0, 256), F.Abs)
+            ad, ma, ne = link(nxt)
+            m["send"](A("wn%d" % t, 0, 256), A("wt_%d" % (t + 1), 0, 256), "arrw%d" % (t + 1), ad, ma, ne)
+        tt(full("fe", 256), full("fi", 256), A("b7", 0, 256), O.mult)
+        ts(full("le", 256), full("code", 256), pc(PARE), O.mult)
+        ts(full("lo", 256), full("code", 256), pc(PARO), O.mult)
+        mm(A("b4", 0, 256), full("rs"), full("fi", 256))
+        act(full("nsel", 256), A("b4", 0, 256), F.Copy, bias=1.0, scale=-1.0)
+        act(full("sel", 256), A("b4", 0, 256), F.Copy)
+        for k in range(16):
+            mm(A("b5", 0, 16), A("sumf", 15 - k, 143 - k), A("fe", k, 256, 16), k == 0, k == 15)
+        for h in range(2):
+            mm(A("b1", 8 * h, 8 * h + 8), A("fi", 128 * h, 128 * h + 128), full("blk8", 8))
+        act(full("ctv", 16), A("b1", 0, 16), F.Copy, acc=full("cs", 1))
+        tt(full("ka", 256), ("ind", KIDS, OL), full("nsel", 256), O.mult)
+        ts(full("el", 16), A("b5", 0, 16), 1536.0, O.add)
+
+        def match(gg):
+            b = "b%d" % ((gg + 2) % 4)
+            lh = "le" if gg % 2 == 0 else "lo"
+            p0 = 32 * (gg // 2)
+            for c0, lp, ln, tri in ((0, 0, 0, True), (128, 0, 128, False), (256, 128, 128, True)):
+                mm(A(b, c0, c0 + 128), A(lh, lp, lp + 128, 1, p0, p0 + 32), A("code", ln, ln + 128, 1, p0, p0 + 32), True, not tri)
+                if tri:
+                    mm(A(b, c0, c0 + 128), full("ident"), full("tri"), False, True)
+            for h, (c0, c1) in enumerate(((0, 256), (256, 384))):
+                o, cv = A("eq", 384 * gg + c0, 384 * gg + c1), A("ctv", 8 * h + gg, 8 * h + gg + 1)
+                if final and gg % 4 == 3:
+                    ts(o, A(b, c0, c1), 12.0, O.is_equal, cv, O.mult)
+                else:
+                    act(o, A(b, c0, c1), F.Relu, bias=NEG11, scale=cv)
+        act(A("b4", 256, 512), full("ka", 256), F.Copy)
+        match(0)
+        tt(full("kb", 256), ("ind", KIDS, full("el", 16)), full("sel", 256), O.mult)
+        tt(full("new", 256), full("kb", 256), A("b4", 256, 512), O.add)
+        if not final:
+            cp(A(co, 0, 256), full("new", 256))
+            ad, ma, ne = link(nxt)
+            m["send"](A(co, 0, 272), A("cw%d" % (t + 1), 0, 272), "arrc%d" % (t + 1), ad, ma, ne)
+            m["landed"](A("wt_%d" % (t + 1), 0, 256), "arrw%d" % (t + 1), ne)
+            m["landed"](A("cw%d" % (t + 1), 0, 272), "arrc%d" % (t + 1), ne)
+        else:
+            ad, ma, ne = link(home)
+            m["send"](full("new", 256), full("yl", 256), "arry", ad, ma, ne)
+            m["landed"](full("yl", 256), "arry", ne)
+        if t == 0:
+            consts3()
+            const_rot(0)
+        tt(full("odm", 16), A("b6", 0, 16), full("dump", 16), O.subtract)
+        cp(A("nap", 0, 16), A("b6", 16, 32))
+        tt(A("nap", 16, 32), A("b6", 16, 32), full("pv", 16), O.mult)
+        for gg in range(1, 8 if final else 5):
+            match(gg)
+        if not final:
+            mm(A("b6", 32, 33), full("onef"), full("cs", 1))
+            cp(A("cint", 0, 1), A("b6", 32, 33))
+
+        def writers():
+            for h in range(2):
+                out = A("b3", 128 * h, 128 * h + 128)
+                for gg in range(8):
+                    lh = A("onesg", 112 - 16 * gg, 240 - 16 * gg)
+                    mm(out, lh, A("eq", 384 * gg + 128 * h, 384 * gg + 128 * h + 128), gg == 0, False)
+                    if h:
+                        mm(out, lh, A("eq", 384 * gg + 256, 384 * gg + 384), False, False)
+                mm(out, full("nblk"), A("fi", 128 * h, 128 * h + 128), False, True)
+
+        def late_w():
+            act(full("wr", 256), A("b3", 0, 256), F.Relu, scale=-1.0 / 16.0)
+            for k in range(16):
+                mm(A("b3", 256, 272), A("sumb", 15 - k, 143 - k), A("wr", k, 256, 16), k == 0, k == 15)
+
+        def late_scatter(final=final):
+            tt(full("wt1", 16), A("b3", 256, 272), full("odm", 16), O.mult)
+            tt(full("wt2", 16), full("wt1", 16), full("dump", 16), O.add)
+            ts(full("wo", 16), full("wt2", 16), 1536.0, O.add)
+            cp(("ind", A("kf", 0, W + L) if final else KALL, full("wo", 16)), full("new", 256))
+        if final:
+            fill(A("kf", W, W + L), 0.0)
+            cp(full("kf", W), KIDS)
+            writers()
+        mm(A("b6", 64, 96), A("rot", 128 * t, 128 * t + 128), full("nap", 32))
+        cp(full("nr", 32), A("b6", 64, 96))
+        if final:
+            late_w()
+            late_scatter()
+        if not final:
+            ts(A("cint", 1, 2), A("cint", 0, 1), 15, O.bitwise_and)
+            ts(A("lim", 0, 1), A("cint", 1, 2), -16.0, O.mult, -1008.0, O.add)
+            build_wx(t + 1)
+            const_rot(t + 1)
+            for gg in range(5, 8):
+                match(gg)
+        for k in range(16):
+            mm(A("b6", 256 + (k - 5 * t) % 16, 512, 16), A("ej", 128 * k, 128 * k + 128), A("nr", 0, 16))
+
+        def late_mount0():
+            act(full("nus", 256), A("b6", 256, 512), F.Copy, bias=1.0, scale=-1.0)
+            tt(full("mt1", 256), A("b6", 256, 512), full("dm", 256), O.mult)
+
+        def late_mount1():
+            tt(full("mt2", 256), full("nus", 256), A("b7", 0, 256), O.mult)
+
+        def late_mount2(t=t, final=final):
+            mm(A("b0", 0, 256), full("ident"), full("mk", 256), True, False)
+            mm(A("b0", 0, 256), full("ident"), full("mt1", 256), False, True)
+            mm(A("b1", 0, 256), full("i16"), full("mt2", 256), True, False)
+            for k in range(16):
+                mm(A("b1", (k - 5 * t) % 16, 256, 16), A("ej", 128 * k, 128 * k + 128), A("nr", 16, 32), False, k == 15)
+            if not final:
+                act(full("mk", 256), A("b0", 0, 256), F.Copy)
+                act(A("b7", 0, 256), A("b1", 0, 256), F.Copy)
+
+        late["w"], late["scatter"], late["mount0"], late["mount1"], late["mount2"] = late_w, late_scatter, late_mount0, late_mount1, late_mount2
+        if not final:
+            writers()
+
+    m["store"]("Y", T.yn[:, :], full("yl", 256), "oyn")
+    for k in range(3):
+        c0, c1 = 512 * k, 512 * k + 512
+        b = "b%d" % (4 + k % 2)
+        act(A(b, 0, 512), A("kf", 1536 + c0, 1536 + c1), F.Copy, scale=2.0)
+        tt(A("ydb", c0, c1), A("kf", c0, c1), A(b, 0, 512), O.add)
+        m["store"]("Y", T.yd[:, c0:c1], A("ydb", c0, c1), "oyd%d" % k)
+        if k == 0:
+            late["mount0"]()
+            late["mount1"]()
+            late["mount2"]()
+        if k == 1:
+            act(full("my", 256), A("b1", 0, 256), F.Copy, scale=64.0, bias=98304.0)
+            tt(full("my2", 256), full("my", 256), A("b0", 0, 256), O.add)
+            m["store"]("Y", T.ymu[:, :], full("my2", 256), "omu")
+    m["finish"]([("arry", link(home)[2])] + [("ld_" + x, 16) for x in LOADS])
+
+
+NEG11 = -11.0
+GWX = 4
+KEY0 = 4
+SCRATCH["nbone"] = ("sbuf", [128, 512], "bfloat16")
+SCRATCH["kf"] = ("sbuf", [128, W + L], "float32")

@@ -12,13 +12,13 @@ SCRATCH = {}
 
 def _buffers():
     for dtype, names in (
-        ("float32", "colf 256 cmf 256 cgf 128 pcol 40 m16 16 w16 16 mw16 16 ct1 128 ct2 128 ct3 128 onef 128 rst 256 dump 16 "
+        ("float32", "colf 256 cmf 256 cgf 128 pcol 40 m16 16 w16 16 ct1 128 ct2 128 onef 128 rst 256 dump 16 "
                     "t64 64 t64b 64 t64c 64 tba 48 tbb 64 kc 256 comp 256 tr 256 sc 256 r16 16 ka 256 kb 256 new 256 ctv 16 cs 1 "
-                    "lim 2 odm 16 wt1 16 wt2 16 my 256 my2 256 yl 256 ydb 1536"),
-        ("bfloat16", "featb 3072 keytab 3072 ntab 3072 tb 3072 mk 256 ident 128 nident 128 selp 144 sumb 144 blk 128 nblk 128 "
-                     "blk8 8 pre 128 rs 128 tri 128 onesg 240 nbias 128 oneb 512 kwf 128 wx 4096 d 4096 da 4096 fs 2048 dm 256 "
-                     "hit 256 fi 256 sel 256 nsel 256 xo 256 code 256 le 256 lo 256 eq 3072 wr 256 nus 256 mt1 256"),
-        ("float16", "last16 256 i16 128 sumf 144 sper 512 g8 144 rot 768 ej 2048 od 32 fe 256 pv 16 nap 32 nr 32 mt2 256"),
+                    "lim 2 odm 16 wt1 16 my 256 yl 256 ydb 1536"),
+        ("bfloat16", "featb 3072 keytab 3072 ntab 3072 tb 3072 mk 256 ident 128 nident 128 selp 144 blk 128 nblk 128 sumb 144 tri 128 onesg 240 wr 256 "
+                     "blk8 8 pre 128 rs 128 nbias 128 oneb 512 kwf 128 wx 4096 d 4096 da 4096 fs 2048 ck 256 "
+                     "hit 256 fi 256 sel 256 nsel 256 xo 256 code 256 lo 256 eq 3072 nus 256 mt1 256"),
+        ("float16", "last16 256 i16 128 back 128 sumf 144 sper 512 g8 144 rot 768 ej 2048 od 32 fe 256 pv 16 nap 32 nr 32 mt2 256"),
         ("int32", "candi 256 kt 3328 mobi 256 lasti 256 wti 1 pint 16 cint 2"),
         ("uint16", "el 16 wo 16"),
     ):
@@ -242,8 +242,12 @@ def rank_program(g, core, T, topo):
     pick(full("tri"), A("oneb", 256, 384), O.is_ge, 0, 1, -1, 128)
 
     iota(full("sc", 256), [[0, 256]], int(BIG), 0)
-    run_pick = m["pick2"]
-    run_pick(full("rst", 256), full("sc", 256), [[0, 16], [1, 16]])
+    m["pick2"](full("rst", 256), full("sc", 256), [[0, 16], [1, 16]])
+    iota(full("onef"), [[0, 128]], 1, 0)
+    iota(full("onesg", 240), [[0, 240]], 1, 0)
+    pick(full("onesg", 240), full("onesg", 240), O.is_ge, -112, 0, 1, 240)
+    pick(full("onesg", 240), full("onesg", 240), O.is_ge, 127, 0, -1, 240)
+    iota(A("kt", W, W + L), [[0, 256]], 0, 0, False)
 
     def pi(k):
         return A("pint", k, k + 1)
@@ -304,10 +308,10 @@ def rank_program(g, core, T, topo):
         fill(full("t64c", 16), 0.5)
         fill(full("t64b", 16), 0.0)
         scan(full("w16", 16), full("t64c", 16), full("t64b", 16), 1.0, O.mult, O.add)
-        tt(full("mw16", 16), full("m16", 16), full("w16", 16), O.mult)
+        tt(full("w16", 16), full("m16", 16), full("w16", 16), O.mult)
         ts(pc(MB), pc(PM), 6.0, O.is_lt)
         ts(pc(CA), pc(PM), 12.0, O.is_lt)
-        red(pc(BS), full("mw16", 16))
+        red(pc(BS), full("w16", 16))
         tt(pc(MA), pc(CA), pc(MB), O.subtract)
         for mul, k, out, mask in ((64.0, 48, "tba", MA), (1.0, 64, "tbb", MB)):
             ts(full("t64", k), full("colf", k), mul, O.mult, 0.5, O.add)
@@ -325,9 +329,9 @@ def rank_program(g, core, T, topo):
         ts(full("ct1"), A("cmf", 0, 128), pc(PM), O.is_gt, 2.0, O.mult)
         ts(full("ct2"), A("cmf", 0, 128), pc(PM), O.is_equal, 1.0, O.mult)
         ts(pc(CA), pc(PM), 11.0, O.is_lt)
-        tt(full("ct3"), full("ct1"), full("ct2"), O.subtract)
+        tt(full("ct1"), full("ct1"), full("ct2"), O.subtract)
         ts(pc(CB), pc(PM), 6.0, O.is_lt)
-        tt(full("pre"), full("ct3"), full("blk"), O.mult)
+        tt(full("pre"), full("ct1"), full("blk"), O.mult)
         ts(full("sumf", 143), full("colf", 143), pc(P1615), O.is_equal, 1.0, O.mult)
         tt(pc(CB), pc(CB), pc(CA), O.subtract)
         ts(A("b7", 0, 256), full("mobi", 256), -1536.0, O.add)
@@ -344,28 +348,29 @@ def rank_program(g, core, T, topo):
     def consts3():
         ts(full("dump", 16), full("colf", 16), 16.0, O.mult, pc(PM), O.add)
         ts(full("dump", 16), full("dump", 16), 1536.0, O.add)
-        ts(full("nblk"), full("blk"), -1.0, O.mult)
-        ts(full("i16"), full("colf"), pc(PF), O.is_equal, 1.0, O.mult)
-        fill(full("onesg", 240), 0.0)
-        fill(A("onesg", 112, 128), 1.0)
-        fill(full("onef"), 1.0)
         ts(A("last16", 0, 256, 1, 0, 8), A("lasti", 0, 256, 1, 0, 8), -1536.0, O.add)
         ts(pc(G15), pc(PF), 16.0, O.mult, 15.0, O.add)
         ts(A("g8", 0, 143, 1, 0, 8), A("colf", 0, 143, 1, 0, 8), A("pcol", G15, G15 + 1, 1, 0, 8), O.is_equal, 1.0, O.mult)
         for k in range(16):
             mm(A("b6", 96, 112), A("g8", 15 - k, 143 - k, 1, 0, 8), A("last16", k, 256, 16, 0, 8), k == 0, k == 15)
-        ts(full("sumb", 143), full("colf", 143), pc(P1615), O.is_equal, 1.0, O.mult)
-        fill(A("kt", W, W + L), 0)
         cp(full("pv", 16), A("b6", 96, 112))
         ts(pc(P16), pc(PG), 16.0, O.mult)
+
+    def consts_ej():
+        ts(full("i16"), full("colf"), pc(PF), O.is_equal, 1.0, O.mult)
         for k in range(16):
             ts(A("ej", 128 * k, 128 * k + 128), full("i16"), A("m16", k, k + 1), O.mult)
 
     def const_rot(t):
-        ts(pi(5), pi(1), float(5 * t), O.add)
-        ts(pi(6), pi(5), 15, O.bitwise_and)
-        tt(pc(PR + t), pi(6), pc(P16), O.add)
-        ts(A("rot", 128 * t, 128 * t + 128), full("colf"), pc(PR + t), O.is_equal, 1.0, O.mult)
+        if t == 0:
+            ts(pi(5), pi(1), 11.0, O.add)
+            ts(pi(6), pi(5), 15, O.bitwise_and)
+            tt(pc(PR), pi(6), pc(P16), O.add)
+            ts(A("rot", 0, 128), full("colf"), pc(PF), O.is_equal, 1.0, O.mult)
+            ts(full("back"), full("colf"), pc(PR), O.is_equal, 1.0, O.mult)
+        else:
+            mm(A("b4", 256, 384), full("back"), A("rot", 128 * t - 128, 128 * t))
+            cp(A("rot", 128 * t, 128 * t + 128), A("b4", 256, 384))
 
     consts_bits()
     ts(pc(WF), full("wti", 1), 1.0, O.mult)
@@ -385,6 +390,9 @@ def rank_program(g, core, T, topo):
     key_a(0)
     key_a(1)
     bit_table(0, 26)
+    act(full("nblk"), full("blk"), F.Copy, scale=-1.0)
+    act(full("sumb", 143), full("selp", 143), F.Copy, scale=1.0 / 16.0)
+    consts_ej()
     key_b(0)
     keytable(2, KEY0)
     FEAT, KEYS, BITS = full("featb", W), full("keytab", W), full("tb", W)
@@ -407,7 +415,9 @@ def rank_program(g, core, T, topo):
             tt(r, ("ind", FEAT, A(cw, l0, l1)), A("wx", 16 * l0, 16 * l1), O.subtract)
             if t == 0 and l0 == 0:
                 keytable(KEY0, 7)
-        ts(full("kc", 256), A(cw, 0, 256), 1.0 / 4096.0, O.mult, pc(KCOL), O.add)
+        if t:
+            late["w"]()
+
         def abs_v(l0, l1):
             act(A("da", 16 * l0, 16 * l1), A("d", 16 * l0, 16 * l1), F.Abs)
             for k in range(16):
@@ -418,7 +428,15 @@ def rank_program(g, core, T, topo):
             mm(c, full("ident"), A("fs", k, 16 * sw, 16), False, True)
         abs_v(*VCH[0])
         if t:
-            late["w"]()
+            late["wl"]()
+            const_rot(t)
+        steps = late["wo"]() if t else iter(())
+        next(steps, None)
+        ts(full("kc", 256), A(cw, 0, 256), 1.0 / 4096.0, O.mult, pc(KCOL), O.add)
+        next(steps, None)
+        if t:
+            ts(full("pv", 16), A(cw, 256, 272), -1536.0, O.add)
+        next(steps, None)
         for k in range(0, 16, kb):
             e = min(k + kb, 16)
             act(A("da", 16 * s0 + sw * k, 16 * s0 + sw * e), A("b%d" % (k // kb), 0, sw * (e - k)), F.Abs)
@@ -429,19 +447,15 @@ def rank_program(g, core, T, topo):
         for c in VCH[1:]:
             abs_v(*c)
         act(A("b6", 0, 128), A("b4", 0, 128), F.Relu, bias=A("lim", 0, 1))
-        if t:
-            ts(full("pv", 16), A(cw, 256, 272), -1536.0, O.add)
-            late["mount0"]()
-        act(A("b3", 0, 128), A("b5", 0, 128), F.Relu, bias=A("lim", 0, 1))
+        act(A("b5", 128, 256), A("b5", 0, 128), F.Relu, bias=A("lim", 0, 1))
         if t == 0:
             bit_table(26, 48)
             consts2()
+        if t:
+            late["mount2"]()
         for h in range(2):
             a, b = 128 * h, 128 * h + 128
-            if t and h:
-                late["mount1"]()
-                late["mount2"]()
-            tt(A("comp", a, b), A("b3", 0, 128) if h else A("b6", 0, 128), A("kc", a, b), O.add)
+            tt(A("comp", a, b), A("b5", 128, 256) if h else A("b6", 0, 128), A("kc", a, b), O.add)
             tr(A("tr", a, b), A("comp", a, b))
             scan(A("sc", a, b), A("rst", a, b), A("tr", a, b), BIG, O.max, O.min)
         best = A("sc", 15, 256, 16)
@@ -453,21 +467,24 @@ def rank_program(g, core, T, topo):
                 k = 2 * dd + bb
                 mm(A("b6", dd, 32, 2), A("sper", 128 * k, 128 * k + 128), A("od", bb, 32, 2), bb == 0, bb == 1)
         ts(OL, A("b6", 0, 16), 1536.0, O.add)
-        tt(full("dm", 256), ("ind", KEYS, OL), full("mk", 256), O.subtract)
+        halves = ((0, 128), (128, 256))
+        for a, b in halves:
+            tt(A("hit", a, b), ("ind", KEYS, A(co, 256 + a // 16, 256 + b // 16)), A("mk", a, b), O.is_equal)
         if not final:
             act(full("xo", 256), ("ind", FEAT, OL), F.Copy)
         act(full("code", 256), ("ind", BITS, OL), F.Copy)
-        ts(full("hit", 256), full("dm", 256), 0.0, O.is_equal)
-        mm(A("b5", 0, 256), full("pre"), full("hit", 256))
-        ts(full("fi", 256), A("b5", 0, 256), 0.0, O.is_lt)
+        for a, b in halves:
+            mm(A("b5" if a == 0 else "b4", 0, 128), full("pre"), A("hit", a, b))
+        for a, b in halves:
+            ts(A("fi", a, b), A("b5" if a == 0 else "b4", 0, 128), 0.0, O.is_lt)
         if not final:
             mm(A("b0", 0, 256), full("ident"), A(wt, 0, 256), True, False)
             mm(A("b0", 0, 256), full("nident"), full("xo", 256), False, True)
             act(A("wn%d" % t, 0, 256), A("b0", 0, 256), F.Abs)
             ad, ma, ne = link(nxt)
             m["send"](A("wn%d" % t, 0, 256), A("wt_%d" % (t + 1), 0, 256), "arrw%d" % (t + 1), ad, ma, ne)
-        tt(full("fe", 256), full("fi", 256), A("b7", 0, 256), O.mult)
-        ts(full("le", 256), full("code", 256), pc(PARE), O.mult)
+        for a, b in halves:
+            tt(A("fe", a, b), A("fi", a, b), A("b7", a, b), O.mult)
         ts(full("lo", 256), full("code", 256), pc(PARO), O.mult)
         mm(A("b4", 0, 256), full("rs"), full("fi", 256))
         act(full("nsel", 256), A("b4", 0, 256), F.Copy, bias=1.0, scale=-1.0)
@@ -482,10 +499,11 @@ def rank_program(g, core, T, topo):
 
         def match(gg):
             b = "b%d" % ((gg + 2) % 4)
-            lh = "le" if gg % 2 == 0 else "lo"
             p0 = 32 * (gg // 2)
+            p1 = p0 + 16 + 16 * (gg % 2)
+            lh = "lo" if gg % 2 else "code"
             for c0, lp, ln, tri in ((0, 0, 0, True), (128, 0, 128, False), (256, 128, 128, True)):
-                mm(A(b, c0, c0 + 128), A(lh, lp, lp + 128, 1, p0, p0 + 32), A("code", ln, ln + 128, 1, p0, p0 + 32), True, not tri)
+                mm(A(b, c0, c0 + 128), A(lh, lp, lp + 128, 1, p0, p1), A("code", ln, ln + 128, 1, p0, p1), True, not tri)
                 if tri:
                     mm(A(b, c0, c0 + 128), full("ident"), full("tri"), False, True)
             for h, (c0, c1) in enumerate(((0, 256), (256, 384))):
@@ -493,13 +511,16 @@ def rank_program(g, core, T, topo):
                 if final and gg % 4 == 3:
                     ts(o, A(b, c0, c1), 12.0, O.is_equal, cv, O.mult)
                 else:
-                    act(o, A(b, c0, c1), F.Relu, bias=NEG11, scale=cv)
+                    act(o, A(b, c0, c1), F.Relu, bias=-11.0, scale=cv)
         act(A("b4", 256, 512), full("ka", 256), F.Copy)
         match(0)
-        tt(full("kb", 256), ("ind", KIDS, full("el", 16)), full("sel", 256), O.mult)
-        tt(full("new", 256), full("kb", 256), A("b4", 256, 512), O.add)
+        for a, b in halves:
+            tt(A("kb", a, b), ("ind", KIDS, A("el", a // 16, b // 16)), A("sel", a, b), O.mult)
+        for a, b in halves:
+            tt(A("new", a, b), A("kb", a, b), A("b4", 256 + a, 256 + b), O.add)
         if not final:
-            cp(A(co, 0, 256), full("new", 256))
+            for a, b in halves:
+                cp(A(co, a, b), A("new", a, b))
             ad, ma, ne = link(nxt)
             m["send"](A(co, 0, 272), A("cw%d" % (t + 1), 0, 272), "arrc%d" % (t + 1), ad, ma, ne)
             m["landed"](A("wt_%d" % (t + 1), 0, 256), "arrw%d" % (t + 1), ne)
@@ -508,21 +529,23 @@ def rank_program(g, core, T, topo):
             ad, ma, ne = link(home)
             m["send"](full("new", 256), full("yl", 256), "arry", ad, ma, ne)
             m["landed"](full("yl", 256), "arry", ne)
+        for gg in range(1, 8 if final else 4):
+            match(gg)
+        act(full("ck", 256), ("ind", KEYS, OL), F.Copy)
+        if not final:
+            match(4)
         if t == 0:
             consts3()
             const_rot(0)
         tt(full("odm", 16), A("b6", 0, 16), full("dump", 16), O.subtract)
         cp(A("nap", 0, 16), A("b6", 16, 32))
         tt(A("nap", 16, 32), A("b6", 16, 32), full("pv", 16), O.mult)
-        for gg in range(1, 8 if final else 5):
-            match(gg)
         if not final:
             mm(A("b6", 32, 33), full("onef"), full("cs", 1))
-            cp(A("cint", 0, 1), A("b6", 32, 33))
 
         def writers():
             for h in range(2):
-                out = A("b3", 128 * h, 128 * h + 128)
+                out = A("b3", 128 * h, 128 + 128 * h)
                 for gg in range(8):
                     lh = A("onesg", 112 - 16 * gg, 240 - 16 * gg)
                     mm(out, lh, A("eq", 384 * gg + 128 * h, 384 * gg + 128 * h + 128), gg == 0, False)
@@ -532,43 +555,51 @@ def rank_program(g, core, T, topo):
 
         def late_w():
             act(full("wr", 256), A("b3", 0, 256), F.Relu, scale=-1.0 / 16.0)
+
+        def late_wl():
             for k in range(16):
                 mm(A("b3", 256, 272), A("sumb", 15 - k, 143 - k), A("wr", k, 256, 16), k == 0, k == 15)
 
-        def late_scatter(final=final):
+        def late_wo():
             tt(full("wt1", 16), A("b3", 256, 272), full("odm", 16), O.mult)
-            tt(full("wt2", 16), full("wt1", 16), full("dump", 16), O.add)
-            ts(full("wo", 16), full("wt2", 16), 1536.0, O.add)
+            yield
+            tt(full("wt1", 16), full("wt1", 16), full("dump", 16), O.add)
+            yield
+            ts(full("wo", 16), full("wt1", 16), 1536.0, O.add)
+            yield
+
+        def late_scatter(final=final):
             cp(("ind", A("kf", 0, W + L) if final else KALL, full("wo", 16)), full("new", 256))
         if final:
-            fill(A("kf", W, W + L), 0.0)
+            iota(A("kf", W, W + L), [[0, 256]], 0, 0)
             cp(full("kf", W), KIDS)
             writers()
         mm(A("b6", 64, 96), A("rot", 128 * t, 128 * t + 128), full("nap", 32))
         cp(full("nr", 32), A("b6", 64, 96))
         if final:
             late_w()
+            late_wl()
+            for _ in late_wo():
+                pass
             late_scatter()
         if not final:
-            ts(A("cint", 1, 2), A("cint", 0, 1), 15, O.bitwise_and)
-            ts(A("lim", 0, 1), A("cint", 1, 2), -16.0, O.mult, -1008.0, O.add)
+            cp(A("cint", 0, 1), A("b6", 32, 33))
             build_wx(t + 1)
-            const_rot(t + 1)
-            for gg in range(5, 8):
-                match(gg)
+            ts(A("cint", 1, 2), A("cint", 0, 1), 15, O.bitwise_and)
         for k in range(16):
-            mm(A("b6", 256 + (k - 5 * t) % 16, 512, 16), A("ej", 128 * k, 128 * k + 128), A("nr", 0, 16))
+            mm(A("b5", (k - 5 * t) % 16, 256, 16), A("ej", 128 * k, 128 * k + 128), A("nr", 0, 16))
+        if not final:
+            match(5)
+        mm(A("b4", 0, 256), full("ident"), full("ck", 256), True, False)
+        mm(A("b4", 0, 256), full("nident"), full("mk", 256), False, True)
 
         def late_mount0():
-            act(full("nus", 256), A("b6", 256, 512), F.Copy, bias=1.0, scale=-1.0)
-            tt(full("mt1", 256), A("b6", 256, 512), full("dm", 256), O.mult)
-
-        def late_mount1():
+            tt(full("mt1", 256), full("nus", 256), A("b4", 0, 256), O.mult)
             tt(full("mt2", 256), full("nus", 256), A("b7", 0, 256), O.mult)
 
-        def late_mount2(t=t, final=final):
-            mm(A("b0", 0, 256), full("ident"), full("mk", 256), True, False)
-            mm(A("b0", 0, 256), full("ident"), full("mt1", 256), False, True)
+        def late_mount2(final=final, t=t):
+            mm(A("b0", 0, 256), full("ident"), full("ck", 256), True, False)
+            mm(A("b0", 0, 256), full("nident"), full("mt1", 256), False, True)
             mm(A("b1", 0, 256), full("i16"), full("mt2", 256), True, False)
             for k in range(16):
                 mm(A("b1", (k - 5 * t) % 16, 256, 16), A("ej", 128 * k, 128 * k + 128), A("nr", 16, 32), False, k == 15)
@@ -576,29 +607,33 @@ def rank_program(g, core, T, topo):
                 act(full("mk", 256), A("b0", 0, 256), F.Copy)
                 act(A("b7", 0, 256), A("b1", 0, 256), F.Copy)
 
-        late["w"], late["scatter"], late["mount0"], late["mount1"], late["mount2"] = late_w, late_scatter, late_mount0, late_mount1, late_mount2
+        late["w"], late["wl"], late["wo"], late["scatter"], late["mount0"], late["mount2"] = (
+            late_w, late_wl, late_wo, late_scatter, late_mount0, late_mount2)
+        act(full("nus", 256), A("b5", 0, 256), F.Copy, bias=1.0, scale=-1.0)
         if not final:
+            match(6)
+            match(7)
+            late_mount0()
+            ts(A("lim", 0, 1), A("cint", 1, 2), -16.0, O.mult, -1008.0, O.add)
             writers()
 
     m["store"]("Y", T.yn[:, :], full("yl", 256), "oyn")
     for k in range(3):
         c0, c1 = 512 * k, 512 * k + 512
-        b = "b%d" % (4 + k % 2)
+        b = "b%d" % (5 + k % 2)
         act(A(b, 0, 512), A("kf", 1536 + c0, 1536 + c1), F.Copy, scale=2.0)
         tt(A("ydb", c0, c1), A("kf", c0, c1), A(b, 0, 512), O.add)
         m["store"]("Y", T.yd[:, c0:c1], A("ydb", c0, c1), "oyd%d" % k)
         if k == 0:
             late["mount0"]()
-            late["mount1"]()
             late["mount2"]()
         if k == 1:
             act(full("my", 256), A("b1", 0, 256), F.Copy, scale=64.0, bias=98304.0)
-            tt(full("my2", 256), full("my", 256), A("b0", 0, 256), O.add)
-            m["store"]("Y", T.ymu[:, :], full("my2", 256), "omu")
+            tt(full("my", 256), full("my", 256), A("b0", 0, 256), O.add)
+            m["store"]("Y", T.ymu[:, :], full("my", 256), "omu")
     m["finish"]([("arry", link(home)[2])] + [("ld_" + x, 16) for x in LOADS])
 
 
-NEG11 = -11.0
 GWX = 4
 KEY0 = 4
 SCRATCH["nbone"] = ("sbuf", [128, 512], "bfloat16")

from concourse.mybir import AluOpType, AxisListType, ActivationFunctionType

W, L, STEPS = 3072, 256, 6
MAGIC = 12582912.0
SCH = (184, 256)
VCH = [(0, 64), (64, 128), (128, 184)]
NVL = SCH[0]
BIG = 1000000.0

SCRATCH = {}


def _buffers():
    for dtype, names in (
        ("float32", "colf 256 cmf 256 cgf 128 pcol 40 m16 16 w16 16 ct1 128 ct2 128 onef 128 rst 256 dump 16 "
                    "t64 64 t64b 64 t64c 64 tba 48 tbb 64 kc 256 comp 256 tr 256 sc 256 r16 16 ka 256 kb 256 new 256 ctv 16 cs 1 "
                    "lim 2 odm 16 wt1 16 my 256 yl 256 ydb 1536"),
        ("bfloat16", "featb 3072 keytab 3072 ntab 3072 tb 3072 mk 256 ident 128 nident 128 selp 144 blk 128 nblk 128 sumb 144 tri 128 onesg 240 wr 256 "
                     "blk8 8 pre 128 rs 128 nbias 128 oneb 512 kwf 128 wx 4096 d 4096 da 4096 fs 2048 ck 256 "
                     "hit 256 fi 256 sel 256 nsel 256 xo 256 code 256 lo 256 eq 3072 nus 256 mt1 256"),
        ("float16", "last16 256 i16 128 back 128 sumf 144 sper 512 g8 144 rot 768 ej 2048 od 32 fe 256 pv 16 nap 32 nr 32 mt2 256"),
        ("int32", "candi 256 kt 3328 mobi 256 lasti 256 wti 1 pint 16 cint 2"),
        ("uint16", "el 16 wo 16"),
    ):
        words = names.split()
        for k in range(0, len(words), 2):
            SCRATCH[words[k]] = ("sbuf", [128, int(words[k + 1])], dtype)
    for t in range(STEPS):
        SCRATCH["cw%d" % t] = ("sbuf", [128, 272], "uint16")
        SCRATCH["co%d" % t] = ("sbuf", [128, 272], "uint16")
        SCRATCH["wt_%d" % t] = ("sbuf", [128, 256], "bfloat16")
        if t < STEPS - 1:
            SCRATCH["wn%d" % t] = ("sbuf", [128, 256], "bfloat16")
    for b in range(8):
        SCRATCH["b%d" % b] = ("psum", [128, 512], "float32")


_buffers()
LOADS = ["cand", "feat0", "feat1", "feat2", "want", "wts", "last", "mkey", "mobj", "kids"]
SEMAPHORES = ["sv", "ss", "sp", "sg", "lsem", "arry", "oyn", "omu"] + ["ld_" + x for x in LOADS] + ["oyd%d" % k for k in range(3)]
SEMAPHORES += ["arrw%d" % k for k in range(1, STEPS)] + ["arrc%d" % k for k in range(1, STEPS)]


def A(name, c0, c1, step=1, p0=0, p1=128):
    return (name, p0, p1, c0, c1, step)


def overlap(a, b):
    if a[1] >= b[2] or b[1] >= a[2] or a[3] >= b[4] or b[3] >= a[4]:
        return False
    if a[5] > 1 and a[5] == b[5] and (a[3] - b[3]) % a[5]:
        return False
    return True


def covers(a, b):
    return a[5] == 1 and a[1] <= b[1] and a[2] >= b[2] and a[3] <= b[3] and a[4] >= b[4]


def machine(g, T):
    q = {"V": g.vector, "S": g.scalar, "P": g.tensor, "G": g, "Y": g.sync}
    sem = {"V": "sv", "S": "ss", "P": "sp", "G": "sg"}
    count = {}
    clock = {e: {} for e in q}
    hist = {}

    def need(e, ent):
        s, v, ck = ent[3], ent[4], ent[5]
        mine = clock[e]
        if mine.get(s, 0) < v:
            q[e].wait_ge(T.sem[s], v)
            for k in ck:
                if mine.get(k, 0) < ck[k]:
                    mine[k] = ck[k]
            if mine.get(s, 0) < v:
                mine[s] = v

    def order(e, R, Wr):
        found = []
        for regs, w in ((R, False), (Wr, True)):
            for r in regs:
                psum = r[0][0] == "b" and r[0][1:].isdigit()
                for ent in hist.get(r[0], []):
                    if (psum and ent[2] != e) or ((w or ent[1]) and overlap(r, ent[0])):
                        found.append(ent)
        found.sort(key=lambda ent: -ent[4])
        for ent in found:
            need(e, ent)

    def log(e, R, Wr, s, v):
        ck = dict(clock[e])
        for regs, w in ((R, False), (Wr, True)):
            for r in regs:
                h = hist.setdefault(r[0], [])
                if w:
                    h[:] = [x for x in h if not covers(r, x[0])]
                h[:] = [x for x in h if not (x[2] == e and x[3] == s and x[0] == r and x[1] == w)]
                h.append([r, w, e, s, v, ck])

    def ap(x):
        if x[0] == "ind":
            return ap(x[1]).indirect(ap(x[2]))
        t = T[x[0]]
        if x[5] == 1:
            return t[x[1]:x[2], x[3]:x[4]]
        return t[x[1]:x[2], x[3]:x[4]:x[5]]

    def run(e, call, R, Wr, acc=False):
        R2, W2 = [], []
        for x in R:
            if isinstance(x, tuple):
                R2 += [x[1], x[2]] if x[0] == "ind" else [x]
        for x in Wr:
            if x[0] == "ind":
                W2.append(x[1])
                R2.append(x[2])
            else:
                W2.append(x)
        order(e, R2, [] if acc else W2)
        if acc:
            for x in W2:
                for ent in hist.get(x[0], []):
                    if ent[2] != e:
                        need(e, ent)
        s = sem[e]
        count[s] = count.get(s, 0) + 1
        call().then_inc(T.sem[s], 1)
        log(e, R2, W2, s, count[s])

    def sc(x):
        return ap(x) if isinstance(x, tuple) else x

    def tt(out, a, b, op):
        run("V", lambda: g.vector.tensor_tensor(ap(out), ap(a), ap(b), op), [a, b], [out])

    def ts(out, a, s1, op0, s2=None, op1=None):
        if op1 is None:
            run("V", lambda: g.vector.tensor_scalar(ap(out), ap(a), sc(s1), None, op0), [a, s1], [out])
        else:
            run("V", lambda: g.vector.tensor_scalar(ap(out), ap(a), sc(s1), sc(s2), op0, op1), [a, s1, s2], [out])

    def cp(out, a):
        run("V", lambda: g.vector.tensor_copy(ap(out), ap(a)), [a], [out])

    def fill(out, c):
        run("V", lambda: g.vector.memset(ap(out), c), [], [out])

    def red(out, a):
        run("V", lambda: g.vector.tensor_reduce(ap(out), ap(a), AxisListType.X, AluOpType.add), [a], [out])

    def scan(out, d0, d1, init, op0, op1):
        run("V", lambda: g.vector.tensor_tensor_scan(ap(out), ap(d0), ap(d1), init, op0, op1), [d0, d1], [out])

    def tr(out, a):
        run("V", lambda: g.vector.transpose(ap(out), ap(a)), [a], [out])

    def act(out, a, func, bias=0.0, scale=1.0, acc=None):
        if acc is None:
            run("S", lambda: g.scalar.activation(ap(out), ap(a), func, bias=sc(bias), scale=sc(scale)), [a, bias, scale], [out])
        else:
            run("S", lambda: g.scalar.activation(ap(out), ap(a), func, bias=sc(bias), scale=sc(scale), accum_out=ap(acc)),
                [a, bias, scale], [out, acc])

    def mm(out, lhsT, rhs, start=True, stop=True):
        run("P", lambda: g.tensor.matmul(ap(out), ap(lhsT), ap(rhs), start, stop), [lhsT, rhs], [out], acc=not start)

    def iota(out, pattern, base, cm, small=True):
        if small:
            run("G", lambda: g.iota(ap(out), pattern, base, cm, allow_small_or_imprecise_dtypes=True), [], [out])
        else:
            run("G", lambda: g.iota(ap(out), pattern, base, cm), [], [out])

    def pick(out, a, op, base, cm, step, n):
        run("G", lambda: g.affine_select(ap(out), ap(a), [[step, n]], op, 0.0, base, cm), [a], [out])

    def pick2(out, a, pattern):
        run("G", lambda: g.affine_select(ap(out), ap(a), pattern, AluOpType.is_equal, 0.0, 0, 0), [a], [out])

    def load(e, out, src, s):
        q[e].dma_start(ap(out), src).then_inc(T.sem[s], 16)
        hist.setdefault(out[0], []).append([out, True, "D", s, 16, {}])

    def store(e, dst, a, s):
        order(e, [a], [])
        q[e].dma_start(dst, ap(a)).then_inc(T.sem[s], 16)
        count[s] = 16

    def landed(out, s, v):
        hist.setdefault(out[0], []).append([out, True, "R", s, v, {}])

    def send(a, out, s, addr, mask, n):
        order("G", [a], [])
        g.remote_dma(ap(out), ap(a), T.sem[s], T.sem["lsem"], addr[1], addr[0], mask)
        count["lsem"] = count.get("lsem", 0) + n

    def finish(extra):
        for s, v in list(count.items()) + extra:
            if clock["G"].get(s, 0) < v:
                g.wait_ge(T.sem[s], v)

    return dict(tt=tt, ts=ts, cp=cp, fill=fill, red=red, scan=scan, tr=tr, act=act, mm=mm, iota=iota, pick=pick, pick2=pick2, load=load,
                store=store, landed=landed, send=send, finish=finish)


def rank_program(g, core, T, topo):
    rank = T.rank_of(core)
    if rank is None:
        return
    O, F = AluOpType, ActivationFunctionType
    m = machine(g, T)
    tt, ts, cp, fill, red, scan, tr, act, mm, iota, pick = (
        m[k] for k in ("tt", "ts", "cp", "fill", "red", "scan", "tr", "act", "mm", "iota", "pick"))
    n = len(T.cores)
    nxt, home = T.cores[(rank + 1) % n], T.cores[(rank - STEPS + 1) % n]

    def link(dst):
        return topo.addr(dst), topo.mask(core, dst), len(topo.engines(core, dst))

    def full(name, w=128):
        return A(name, 0, w)

    load = m["load"]
    load("S", full("wti", 1), T.wts[:, :], "ld_wts")
    load("Y", full("candi", 256), T.cand[:, :], "ld_cand")
    load("S", full("wt_0", 256), T.want[:, :], "ld_want")
    for k in range(3):
        load("Y", A("featb", 1024 * k, 1024 * k + 1024), T.feat[:, 1024 * k:1024 * k + 1024], "ld_feat%d" % k)
    load("S", A("lasti", 0, 256, 1, 0, 8), T.last[:, :], "ld_last")
    load("S", full("mk", 256), T.mkey[:, :], "ld_mkey")
    load("S", full("mobi", 256), T.mobj[:, :], "ld_mobj")
    load("Y", A("kt", 0, W), T.kids[:, :], "ld_kids")

    iota(full("pint", 1), [[0, 1]], 0, 1, False)
    iota(full("cgf", 128), [[1, 8], [0, 16]], 0, 0)
    iota(full("colf", 256), [[1, 256]], 0, 0)
    iota(full("oneb", 128), [[0, 128]], 1, 0)
    pick(full("ident"), full("oneb"), O.is_equal, 0, 1, -1, 128)
    iota(full("cmf", 256), [[0, 16], [1, 16]], 0, 0)
    iota(A("oneb", 128, 256), [[0, 128]], -1, 0)
    pick(full("nident"), A("oneb", 128, 256), O.is_equal, 0, 1, -1, 128)
    iota(A("oneb", 256, 384), [[0, 128]], -16, 0)
    pick(full("tri"), A("oneb", 256, 384), O.is_ge, 0, 1, -1, 128)

    iota(full("sc", 256), [[0, 256]], int(BIG), 0)
    m["pick2"](full("rst", 256), full("sc", 256), [[0, 16], [1, 16]])
    iota(full("onef"), [[0, 128]], 1, 0)
    iota(full("onesg", 240), [[0, 240]], 1, 0)
    pick(full("onesg", 240), full("onesg", 240), O.is_ge, -112, 0, 1, 240)
    pick(full("onesg", 240), full("onesg", 240), O.is_ge, 127, 0, -1, 240)
    iota(A("kt", W, W + L), [[0, 256]], 0, 0, False)

    def pi(k):
        return A("pint", k, k + 1)

    def pc(k):
        return A("pcol", k, k + 1)
    PF, PM, PG, P16, P1615, HA, HB, PP16, PM16, KCOL, CA, CB, PARE, PARO, BS, MA, MB, WF, WF64, G15 = range(20)
    PR = 24
    ts(pi(2), pi(0), 4, O.arith_shift_right)
    ts(pi(1), pi(0), 15, O.bitwise_and)
    cp(pc(PG), pi(2))
    cp(pc(PM), pi(1))
    cp(pc(PF), pi(0))
    ts(full("blk"), full("cgf"), pc(PG), O.is_equal, 1.0, O.mult)
    ts(pc(P1615), pc(PG), 16.0, O.mult, 15.0, O.add)
    ts(full("selp", 143), full("colf", 143), pc(P1615), O.is_equal, 16.0, O.mult)

    def build_wx(t):
        for k in range(16):
            out, src = A("wx", k, 16 * NVL, 16), A("wt_%d" % t, 0, NVL)
            if t and k >= 16 - GWX:
                pick(out, src, O.is_ge, 1, 0, 0, NVL)
            else:
                cp(out, src)

    def key_a(k):
        b, c, x, z = A("b%d" % k, 0, 512), A("featb", 512 * k, 512 * k + 512), A("ntab", 512 * k, 512 * k + 512), A("kf", 512 * k, 512 * k + 512)
        if k < 3:
            mm(b, full("kwf"), c)
            act(z, b, F.Copy, bias=-31.5)
        else:
            z = b
            mm(b, full("kwf"), c, True, False)
            mm(b, A("nbias", 0, 128, 1, 0, 1), A("nbone", 0, 512, 1, 0, 1), False, True)
        ts(x, z, 64.0 * MAGIC, O.add, 64.0 * MAGIC, O.subtract)

    def key_b(k):
        b, c, x = A("b%d" % k, 0, 512), A("featb", 512 * k, 512 * k + 512), A("ntab", 512 * k, 512 * k + 512)
        mm(b, full("kwf"), c, True, False)
        mm(b, full("nident"), x, False, True)
        act(A("keytab", 512 * k, 512 * k + 512), b, F.Copy)

    def consts1():
        ts(pc(KCOL), pc(PM), 0.625, O.add)
        fill(A("lim", 0, 1), -1008.0)
        ts(pi(3), pi(0), 16, O.bitwise_and)
        ts(pc(PP16), pc(PF), 16.0, O.add)
        ts(pc(PM16), pc(PF), -16.0, O.add)
        ts(pc(HB), pi(3), 256.0, O.mult)
        ts(pc(HA), pc(HB), -1.0, O.mult, 4096.0, O.add)
        ts(A("sper", 256, 384), full("colf"), pc(PM16), O.is_equal, pc(HB), O.mult)
        ts(A("sper", 384, 512), full("colf"), pc(PF), O.is_equal, pc(HB), O.mult)
        ts(A("sper", 0, 128), full("colf"), pc(PF), O.is_equal, pc(HA), O.mult)
        ts(A("sper", 128, 256), full("colf"), pc(PP16), O.is_equal, pc(HA), O.mult)

    def consts_bits():
        ts(full("m16", 16), full("colf", 16), pc(PM), O.is_equal, 1.0, O.mult)
        fill(full("t64c", 16), 0.5)
        fill(full("t64b", 16), 0.0)
        scan(full("w16", 16), full("t64c", 16), full("t64b", 16), 1.0, O.mult, O.add)
        tt(full("w16", 16), full("m16", 16), full("w16", 16), O.mult)
        ts(pc(MB), pc(PM), 6.0, O.is_lt)
        ts(pc(CA), pc(PM), 12.0, O.is_lt)
        red(pc(BS), full("w16", 16))
        tt(pc(MA), pc(CA), pc(MB), O.subtract)
        for mul, k, out, mask in ((64.0, 48, "tba", MA), (1.0, 64, "tbb", MB)):
            ts(full("t64", k), full("colf", k), mul, O.mult, 0.5, O.add)
            ts(full("t64", k), full("t64", k), pc(BS), O.mult)
            ts(full("t64b", k), full("t64", k), MAGIC, O.add, MAGIC, O.subtract)
            tt(full("t64c", k), full("t64", k), full("t64b", k), O.subtract)
            ts(full("t64c", k), full("t64c", k), 0.0, O.is_gt, 2.0, O.mult)
            ts(full(out, k), full("t64c", k), -1.0, O.add, pc(mask), O.mult)

    def bit_table(k0, k1):
        for k in range(k0, k1):
            act(A("tb", 64 * k, 64 * k + 64), full("tbb", 64), F.Identity, bias=A("tba", k, k + 1))

    def consts2():
        ts(full("ct1"), A("cmf", 0, 128), pc(PM), O.is_gt, 2.0, O.mult)
        ts(full("ct2"), A("cmf", 0, 128), pc(PM), O.is_equal, 1.0, O.mult)
        ts(pc(CA), pc(PM), 11.0, O.is_lt)
        tt(full("ct1"), full("ct1"), full("ct2"), O.subtract)
        ts(pc(CB), pc(PM), 6.0, O.is_lt)
        tt(full("pre"), full("ct1"), full("blk"), O.mult)
        ts(full("sumf", 143), full("colf", 143), pc(P1615), O.is_equal, 1.0, O.mult)
        tt(pc(CB), pc(CB), pc(CA), O.subtract)
        ts(A("b7", 0, 256), full("mobi", 256), -1536.0, O.add)
        ts(pc(CB), pc(CB), 1.0, O.add)
        ts(full("ct1"), A("cmf", 0, 128), 8.0, O.is_lt)
        tt(pc(CA), pc(CA), pc(CB), O.subtract)
        ts(full("ct2"), full("ct1"), pc(CA), O.mult, pc(CB), O.add)
        ts(full("blk8", 8), full("colf", 8), pc(PG), O.is_equal, 1.0, O.mult)
        ts(pi(4), pi(2), 1, O.bitwise_and)
        tt(full("rs"), full("ct2"), full("blk"), O.mult)
        ts(pc(PARO), pi(4), 1.0, O.mult)
        ts(pc(PARE), pc(PARO), -1.0, O.mult, 1.0, O.add)

    def consts3():
        ts(full("dump", 16), full("colf", 16), 16.0, O.mult, pc(PM), O.add)
        ts(full("dump", 16), full("dump", 16), 1536.0, O.add)
        ts(A("last16", 0, 256, 1, 0, 8), A("lasti", 0, 256, 1, 0, 8), -1536.0, O.add)
        ts(pc(G15), pc(PF), 16.0, O.mult, 15.0, O.add)
        ts(A("g8", 0, 143, 1, 0, 8), A("colf", 0, 143, 1, 0, 8), A("pcol", G15, G15 + 1, 1, 0, 8), O.is_equal, 1.0, O.mult)
        for k in range(16):
            mm(A("b6", 96, 112), A("g8", 15 - k, 143 - k, 1, 0, 8), A("last16", k, 256, 16, 0, 8), k == 0, k == 15)
        cp(full("pv", 16), A("b6", 96, 112))
        ts(pc(P16), pc(PG), 16.0, O.mult)

    def consts_ej():
        ts(full("i16"), full("colf"), pc(PF), O.is_equal, 1.0, O.mult)
        for k in range(16):
            ts(A("ej", 128 * k, 128 * k + 128), full("i16"), A("m16", k, k + 1), O.mult)

    def const_rot(t):
        if t == 0:
            ts(pi(5), pi(1), 11.0, O.add)
            ts(pi(6), pi(5), 15, O.bitwise_and)
            tt(pc(PR), pi(6), pc(P16), O.add)
            ts(A("rot", 0, 128), full("colf"), pc(PF), O.is_equal, 1.0, O.mult)
            ts(full("back"), full("colf"), pc(PR), O.is_equal, 1.0, O.mult)
        else:
            mm(A("b4", 256, 384), full("back"), A("rot", 128 * t - 128, 128 * t))
            cp(A("rot", 128 * t, 128 * t + 128), A("b4", 256, 384))

    consts_bits()
    ts(pc(WF), full("wti", 1), 1.0, O.mult)
    ts(full("kwf"), full("blk"), pc(WF), O.mult)
    cp(A("cw0", 0, 256), full("candi", 256))
    build_wx(0)
    consts1()
    fill(A("nbias", 0, 128, 1, 0, 1), -31.5)
    fill(A("nbone", 0, 512, 1, 0, 1), 1.0)

    def keytable(k0, k1):
        for k in range(k0, k1):
            if k < 6:
                key_a(k)
            if k:
                key_b(k - 1)
    key_a(0)
    key_a(1)
    bit_table(0, 26)
    act(full("nblk"), full("blk"), F.Copy, scale=-1.0)
    act(full("sumb", 143), full("selp", 143), F.Copy, scale=1.0 / 16.0)
    consts_ej()
    key_b(0)
    keytable(2, KEY0)
    FEAT, KEYS, BITS = full("featb", W), full("keytab", W), full("tb", W)
    KIDS, KALL = A("kt", 0, W), A("kt", 0, W + L)
    late = {}

    def dist_to(l0, l1):
        return A("b4", l0, l1) if l1 <= 128 else A("b5", l0 - 128, l1 - 128)

    for t in range(STEPS):
        cw, wt, co = "cw%d" % t, "wt_%d" % t, "co%d" % t
        final = t == STEPS - 1
        OL = A(co, 256, 272)
        s0, s1 = SCH
        sw = s1 - s0
        kb = 512 // sw
        act(A("fs", 0, 16 * sw), ("ind", FEAT, A(cw, s0, s1)), F.Copy)
        for l0, l1 in VCH:
            r = A("d", 16 * l0, 16 * l1)
            tt(r, ("ind", FEAT, A(cw, l0, l1)), A("wx", 16 * l0, 16 * l1), O.subtract)
            if t == 0 and l0 == 0:
                keytable(KEY0, 7)
        if t:
            late["w"]()

        def abs_v(l0, l1):
            act(A("da", 16 * l0, 16 * l1), A("d", 16 * l0, 16 * l1), F.Abs)
            for k in range(16):
                mm(dist_to(l0, l1), A("selp", 15 - k, 143 - k), A("da", 16 * l0 + k, 16 * l1, 16), k == 0, k == 15)
        for k in range(16):
            c = A("b%d" % (k // kb), (k % kb) * sw, (k % kb) * sw + sw)
            mm(c, full("nident"), A(wt, s0, s1), True, False)
            mm(c, full("ident"), A("fs", k, 16 * sw, 16), False, True)
        abs_v(*VCH[0])
        if t:
            late["wl"]()
            const_rot(t)
        steps = late["wo"]() if t else iter(())
        next(steps, None)
        ts(full("kc", 256), A(cw, 0, 256), 1.0 / 4096.0, O.mult, pc(KCOL), O.add)
        next(steps, None)
        if t:
            ts(full("pv", 16), A(cw, 256, 272), -1536.0, O.add)
        next(steps, None)
        for k in range(0, 16, kb):
            e = min(k + kb, 16)
            act(A("da", 16 * s0 + sw * k, 16 * s0 + sw * e), A("b%d" % (k // kb), 0, sw * (e - k)), F.Abs)
        for k in range(16):
            mm(dist_to(s0, s1), A("selp", 15 - k, 143 - k), A("da", 16 * s0 + sw * k, 16 * s0 + sw * k + sw), k == 0, k == 15)
        if t:
            late["scatter"]()
        for c in VCH[1:]:
            abs_v(*c)
        act(A("b6", 0, 128), A("b4", 0, 128), F.Relu, bias=A("lim", 0, 1))
        act(A("b5", 128, 256), A("b5", 0, 128), F.Relu, bias=A("lim", 0, 1))
        if t == 0:
            bit_table(26, 48)
            consts2()
        if t:
            late["mount2"]()
        for h in range(2):
            a, b = 128 * h, 128 * h + 128
            tt(A("comp", a, b), A("b5", 128, 256) if h else A("b6", 0, 128), A("kc", a, b), O.add)
            tr(A("tr", a, b), A("comp", a, b))
            scan(A("sc", a, b), A("rst", a, b), A("tr", a, b), BIG, O.max, O.min)
        best = A("sc", 15, 256, 16)
        ts(full("r16", 16), best, MAGIC, O.add, MAGIC, O.subtract)
        ts(A("od", 16, 32), best, 16.5, O.is_ge, 1.0 / 4096.0, O.mult)
        tt(A("od", 0, 16), best, full("r16", 16), O.subtract)
        for dd in range(2):
            for bb in range(2):
                k = 2 * dd + bb
                mm(A("b6", dd, 32, 2), A("sper", 128 * k, 128 * k + 128), A("od", bb, 32, 2), bb == 0, bb == 1)
        ts(OL, A("b6", 0, 16), 1536.0, O.add)
        halves = ((0, 128), (128, 256))
        for a, b in halves:
            tt(A("hit", a, b), ("ind", KEYS, A(co, 256 + a // 16, 256 + b // 16)), A("mk", a, b), O.is_equal)
        if not final:
            act(full("xo", 256), ("ind", FEAT, OL), F.Copy)
        act(full("code", 256), ("ind", BITS, OL), F.Copy)
        for a, b in halves:
            mm(A("b5" if a == 0 else "b4", 0, 128), full("pre"), A("hit", a, b))
        for a, b in halves:
            ts(A("fi", a, b), A("b5" if a == 0 else "b4", 0, 128), 0.0, O.is_lt)
        if not final:
            mm(A("b0", 0, 256), full("ident"), A(wt, 0, 256), True, False)
            mm(A("b0", 0, 256), full("nident"), full("xo", 256), False, True)
            act(A("wn%d" % t, 0, 256), A("b0", 0, 256), F.Abs)
            ad, ma, ne = link(nxt)
            m["send"](A("wn%d" % t, 0, 256), A("wt_%d" % (t + 1), 0, 256), "arrw%d" % (t + 1), ad, ma, ne)
        for a, b in halves:
            tt(A("fe", a, b), A("fi", a, b), A("b7", a, b), O.mult)
        ts(full("lo", 256), full("code", 256), pc(PARO), O.mult)
        mm(A("b4", 0, 256), full("rs"), full("fi", 256))
        act(full("nsel", 256), A("b4", 0, 256), F.Copy, bias=1.0, scale=-1.0)
        act(full("sel", 256), A("b4", 0, 256), F.Copy)
        for k in range(16):
            mm(A("b5", 0, 16), A("sumf", 15 - k, 143 - k), A("fe", k, 256, 16), k == 0, k == 15)
        for h in range(2):
            mm(A("b1", 8 * h, 8 * h + 8), A("fi", 128 * h, 128 * h + 128), full("blk8", 8))
        act(full("ctv", 16), A("b1", 0, 16), F.Copy, acc=full("cs", 1))
        tt(full("ka", 256), ("ind", KIDS, OL), full("nsel", 256), O.mult)
        ts(full("el", 16), A("b5", 0, 16), 1536.0, O.add)

        def match(gg):
            b = "b%d" % ((gg + 2) % 4)
            p0 = 32 * (gg // 2)
            p1 = p0 + 16 + 16 * (gg % 2)
            lh = "lo" if gg % 2 else "code"
            for c0, lp, ln, tri in ((0, 0, 0, True), (128, 0, 128, False), (256, 128, 128, True)):
                mm(A(b, c0, c0 + 128), A(lh, lp, lp + 128, 1, p0, p1), A("code", ln, ln + 128, 1, p0, p1), True, not tri)
                if tri:
                    mm(A(b, c0, c0 + 128), full("ident"), full("tri"), False, True)
            for h, (c0, c1) in enumerate(((0, 256), (256, 384))):
                o, cv = A("eq", 384 * gg + c0, 384 * gg + c1), A("ctv", 8 * h + gg, 8 * h + gg + 1)
                if final and gg % 4 == 3:
                    ts(o, A(b, c0, c1), 12.0, O.is_equal, cv, O.mult)
                else:
                    act(o, A(b, c0, c1), F.Relu, bias=-11.0, scale=cv)
        act(A("b4", 256, 512), full("ka", 256), F.Copy)
        match(0)
        for a, b in halves:
            tt(A("kb", a, b), ("ind", KIDS, A("el", a // 16, b // 16)), A("sel", a, b), O.mult)
        for a, b in halves:
            tt(A("new", a, b), A("kb", a, b), A("b4", 256 + a, 256 + b), O.add)
        if not final:
            for a, b in halves:
                cp(A(co, a, b), A("new", a, b))
            ad, ma, ne = link(nxt)
            m["send"](A(co, 0, 272), A("cw%d" % (t + 1), 0, 272), "arrc%d" % (t + 1), ad, ma, ne)
            m["landed"](A("wt_%d" % (t + 1), 0, 256), "arrw%d" % (t + 1), ne)
            m["landed"](A("cw%d" % (t + 1), 0, 272), "arrc%d" % (t + 1), ne)
        else:
            ad, ma, ne = link(home)
            m["send"](full("new", 256), full("yl", 256), "arry", ad, ma, ne)
            m["landed"](full("yl", 256), "arry", ne)
        for gg in range(1, 8 if final else 4):
            match(gg)
        act(full("ck", 256), ("ind", KEYS, OL), F.Copy)
        if not final:
            match(4)
        if t == 0:
            consts3()
            const_rot(0)
        tt(full("odm", 16), A("b6", 0, 16), full("dump", 16), O.subtract)
        cp(A("nap", 0, 16), A("b6", 16, 32))
        tt(A("nap", 16, 32), A("b6", 16, 32), full("pv", 16), O.mult)
        if not final:
            mm(A("b6", 32, 33), full("onef"), full("cs", 1))

        def writers():
            for h in range(2):
                out = A("b3", 128 * h, 128 + 128 * h)
                for gg in range(8):
                    lh = A("onesg", 112 - 16 * gg, 240 - 16 * gg)
                    mm(out, lh, A("eq", 384 * gg + 128 * h, 384 * gg + 128 * h + 128), gg == 0, False)
                    if h:
                        mm(out, lh, A("eq", 384 * gg + 256, 384 * gg + 384), False, False)
                mm(out, full("nblk"), A("fi", 128 * h, 128 * h + 128), False, True)

        def late_w():
            act(full("wr", 256), A("b3", 0, 256), F.Relu, scale=-1.0 / 16.0)

        def late_wl():
            for k in range(16):
                mm(A("b3", 256, 272), A("sumb", 15 - k, 143 - k), A("wr", k, 256, 16), k == 0, k == 15)

        def late_wo():
            tt(full("wt1", 16), A("b3", 256, 272), full("odm", 16), O.mult)
            yield
            tt(full("wt1", 16), full("wt1", 16), full("dump", 16), O.add)
            yield
            ts(full("wo", 16), full("wt1", 16), 1536.0, O.add)
            yield

        def late_scatter(final=final):
            cp(("ind", A("kf", 0, W + L) if final else KALL, full("wo", 16)), full("new", 256))
        if final:
            iota(A("kf", W, W + L), [[0, 256]], 0, 0)
            cp(full("kf", W), KIDS)
            writers()
        mm(A("b6", 64, 96), A("rot", 128 * t, 128 * t + 128), full("nap", 32))
        cp(full("nr", 32), A("b6", 64, 96))
        if final:
            late_w()
            late_wl()
            for _ in late_wo():
                pass
            late_scatter()
        if not final:
            cp(A("cint", 0, 1), A("b6", 32, 33))
            build_wx(t + 1)
            ts(A("cint", 1, 2), A("cint", 0, 1), 15, O.bitwise_and)
        for k in range(16):
            mm(A("b5", (k - 5 * t) % 16, 256, 16), A("ej", 128 * k, 128 * k + 128), A("nr", 0, 16))
        if not final:
            match(5)
        mm(A("b4", 0, 256), full("ident"), full("ck", 256), True, False)
        mm(A("b4", 0, 256), full("nident"), full("mk", 256), False, True)

        def late_mount0():
            tt(full("mt1", 256), full("nus", 256), A("b4", 0, 256), O.mult)
            tt(full("mt2", 256), full("nus", 256), A("b7", 0, 256), O.mult)

        def late_mount2(final=final, t=t):
            mm(A("b0", 0, 256), full("ident"), full("ck", 256), True, False)
            mm(A("b0", 0, 256), full("nident"), full("mt1", 256), False, True)
            mm(A("b1", 0, 256), full("i16"), full("mt2", 256), True, False)
            for k in range(16):
                mm(A("b1", (k - 5 * t) % 16, 256, 16), A("ej", 128 * k, 128 * k + 128), A("nr", 16, 32), False, k == 15)
            if not final:
                act(full("mk", 256), A("b0", 0, 256), F.Copy)
                act(A("b7", 0, 256), A("b1", 0, 256), F.Copy)

        late["w"], late["wl"], late["wo"], late["scatter"], late["mount0"], late["mount2"] = (
            late_w, late_wl, late_wo, late_scatter, late_mount0, late_mount2)
        act(full("nus", 256), A("b5", 0, 256), F.Copy, bias=1.0, scale=-1.0)
        if not final:
            match(6)
            match(7)
            late_mount0()
            ts(A("lim", 0, 1), A("cint", 1, 2), -16.0, O.mult, -1008.0, O.add)
            writers()

    m["store"]("Y", T.yn[:, :], full("yl", 256), "oyn")
    for k in range(3):
        c0, c1 = 512 * k, 512 * k + 512
        b = "b%d" % (5 + k % 2)
        act(A(b, 0, 512), A("kf", 1536 + c0, 1536 + c1), F.Copy, scale=2.0)
        tt(A("ydb", c0, c1), A("kf", c0, c1), A(b, 0, 512), O.add)
        m["store"]("Y", T.yd[:, c0:c1], A("ydb", c0, c1), "oyd%d" % k)
        if k == 0:
            late["mount0"]()
            late["mount2"]()
        if k == 1:
            act(full("my", 256), A("b1", 0, 256), F.Copy, scale=64.0, bias=98304.0)
            tt(full("my", 256), full("my", 256), A("b0", 0, 256), O.add)
            m["store"]("Y", T.ymu[:, :], full("my", 256), "omu")
    m["finish"]([("arry", link(home)[2])] + [("ld_" + x, 16) for x in LOADS])


GWX = 4
KEY0 = 4
SCRATCH["nbone"] = ("sbuf", [128, 512], "bfloat16")
SCRATCH["kf"] = ("sbuf", [128, W + L], "float32")
